import numpy as np
import ml_dtypes


def mxq(x, axis, fmt="e4m3"):
    dtype, down = {"e4m3": (ml_dtypes.float8_e4m3fn, 7), "e5m2": (ml_dtypes.float8_e5m2, 14)}[fmt]
    v = np.moveaxis(np.asarray(x, np.float32).astype(ml_dtypes.bfloat16).astype(np.float64), axis, -1)
    blocks = v.reshape(v.shape[:-1] + (-1, 32))
    amax = np.abs(blocks).max(-1, keepdims=True)
    byte = np.maximum(np.where(amax > 0, np.frexp(amax)[1] - 1 + 127, 0) - down, 1)
    scale = np.exp2(byte - 127.0)
    codes = (blocks / scale).astype(np.float32).astype(dtype).astype(np.float64)
    return np.moveaxis((codes * scale).reshape(v.shape), -1, axis)


WIDE = False


def mx_kscale(k):
    if not WIDE:
        return np.ones(k)
    levels = np.array([10, -10, 5, -5, 0])
    if k % 512:
        return np.exp2(np.random.permutation(np.resize(levels, k // 32))).repeat(32)
    a = np.empty((k // 512, 16))
    for p in range(k // 512):
        a[p, :8] = np.random.permutation(np.resize(levels, 8))
        for g in range(8):
            far = levels[np.abs(levels - a[p, g]) >= 10]
            a[p, g + 8] = far[np.random.randint(len(far))]
    return np.exp2(a.ravel()).repeat(32)


def f64(x):
    return np.asarray(x).astype(np.float64)


def striped(idx):
    return np.tile(idx.reshape(-1, 16).T, (8, 1)).astype(np.uint16)


def unstriped(offs):
    return offs[:16].T.reshape(-1).astype(np.int64)


def pack_weight(w):
    k, n = w.shape
    w = f64(np.asarray(w, np.float32).astype(ml_dtypes.bfloat16)).reshape(k // 32, 32, n)
    amax = np.abs(w).max(1)
    byte = np.clip(np.where(amax > 0, np.frexp(amax)[1] - 1 + 127 - 7, 1), 1, 254)
    scaled = (w * np.exp2(127.0 - byte)[:, None, :]).reshape(k, n).astype(np.float32)
    words = np.ascontiguousarray(scaled.reshape(k // 512, 128, 4, n).transpose(0, 1, 3, 2)).astype(ml_dtypes.float8_e4m3fn).view(np.uint8)
    return words, np.ascontiguousarray(byte.astype(np.uint8).reshape(k // 512, 16, n))


def unpack_weight(words, scales):
    g, p, n, _ = words.shape
    vals = np.ascontiguousarray(words).view(ml_dtypes.float8_e4m3fn).astype(np.float64) * np.repeat(np.exp2(scales.astype(np.float64) - 127.0), 8, axis=1)[..., None]
    return vals.transpose(0, 1, 3, 2).reshape(g * 512, n)


def planes(y):
    n, m = y.shape
    v = y.astype(np.float32).astype(ml_dtypes.bfloat16).astype(np.float64).reshape(n // 32, 32, m)
    top = np.abs(v).max(1)
    byte = np.clip(np.where(top > 0, np.frexp(top)[1] - 1 + 127 - 7, 1), 1, 254)
    codes = (v * np.exp2(127.0 - byte)[:, None, :]).reshape(n, m).astype(np.float32).astype(ml_dtypes.float8_e4m3fn).view(np.uint8)
    words = codes.reshape(n // 512, 128, 4, m).transpose(0, 1, 3, 2)
    return np.ascontiguousarray(words), np.ascontiguousarray(byte.astype(np.uint8).reshape(n // 512, 16, m))


def relu(v):
    return np.maximum(v, 0.0)


K, T, S, D, V, N = 1024, 1024, 512, 3, 256, 512
P = 2 ** 7


def setup_inputs():
    n = np.random.standard_normal
    s = mx_kscale(K)[:, None]
    near = np.random.permutation(S)
    packed_xT = pack_weight(n((K, T)) * s)
    return {
        "x_words": packed_xT[0],
        "x_scales": packed_xT[1],
        "w1": (n((K, N)) / np.sqrt(K) / s).astype(np.float32),
        "w2": (n((K, N)) / np.sqrt(K) / s).astype(np.float32),
        "w3": (n((K, N)) / np.sqrt(K) / s).astype(np.float32),
        "corr": (np.tile(np.random.uniform(0.0, 1.0, (9, 1, V)) / np.sqrt(D), (1, P, 1))).astype(np.float32),
        "offs": striped(np.random.permutation(T)[:S]),
        "pos1": striped(near[:V]),
        "pos2": striped(near[V:]),
        "pos3": striped(np.random.permutation(S)[:V]),
    }


def reference(x_words, x_scales, w1, w2, w3, corr, offs, pos1, pos2, pos3):
    xq = unpack_weight(x_words, x_scales)[:, unstriped(offs)]
    y0 = mxq(f64(w1), 0, "e4m3").T @ xq
    y1 = mxq(f64(w2), 0, "e4m3").T @ xq
    y2 = mxq(f64(w3), 0, "e4m3").T @ xq
    out_0 = relu(y0[:, unstriped(pos1)] * f64(corr)[0, :1] + y0[:, unstriped(pos2)] * f64(corr)[1, :1] + y0[:, unstriped(pos3)] * f64(corr)[2, :1] + y1[:, unstriped(pos1)] * f64(corr)[3, :1] + y1[:, unstriped(pos2)] * f64(corr)[4, :1] + y1[:, unstriped(pos3)] * f64(corr)[5, :1] + y2[:, unstriped(pos1)] * f64(corr)[6, :1] + y2[:, unstriped(pos2)] * f64(corr)[7, :1] + y2[:, unstriped(pos3)] * f64(corr)[8, :1])
    return (out_0,) + planes(out_0)

@@ -1,0 +1,244 @@
+from contextlib import ExitStack
+
+import concourse.mybir as mybir
+from concourse.masks import make_identity
+
+F32 = mybir.dt.float32
+BF16 = mybir.dt.bfloat16
+I32 = mybir.dt.int32
+U32 = mybir.dt.uint32
+U16 = mybir.dt.uint16
+U8 = mybir.dt.uint8
+FP8X4 = mybir.dt.float8_e4m3fn_x4
+RELU = mybir.ActivationFunctionType.Relu
+MULT = mybir.AluOpType.mult
+
+K, T, S, D, V, N = 1024, 1024, 512, 3, 256, 512
+P = 128
+PACK = 4
+PASSES = K // (P * PACK)
+CHUNKS = N // P
+HALVES = V // P
+FLOPS = 2 * K * N * S * D
+
+LOADS = [[(0, 128), (128, 256), (256, 384), (384, 512)], [(0, 256), (256, 512)], [(0, 256), (256, 512)]]
+BEHIND = {(0, 0): (1, 1), (1, 0): (2, 1), (1, 2): (3, 1), (2, 1): (4, 0), (2, 2): (4, 1), (4, 1): (6, 0), (4, 2): (6, 1),
+          (6, 1): (8, 0), (6, 2): (8, 1), (8, 1): (10, 0), (8, 2): (10, 1)}
+
+
+def tile_picked_zkp_three_po_kernel(tc, x_words, x_scales, w1, w2, w3, corr, offs, pos1, pos2, pos3, out_0, out_1, out_2):
+    nc = tc.nc
+    weights = [w1, w2, w3]
+    with ExitStack() as ctx:
+        lists = ctx.enter_context(tc.tile_pool(name="lists", bufs=1))
+        keep = ctx.enter_context(tc.tile_pool(name="keep", bufs=1))
+        ring = ctx.enter_context(tc.tile_pool(name="ring", bufs=3))
+        rows = ctx.enter_context(tc.tile_pool(name="rows", bufs=4))
+        prods = ctx.enter_context(tc.tile_pool(name="prods", bufs=6))
+        ybanks = ctx.enter_context(tc.psum_pool(name="ybanks", bufs=4))
+        banks = ctx.enter_context(tc.psum_pool(name="banks", bufs=1))
+
+        offs_t = lists.tile([P, S // 16], U16, name="offs_t")
+        pos_t = [lists.tile([P, V // 16], U16, name="pos_t%d" % d) for d in range(D)]
+        x_all = [keep.tile([P, T], I32, name="x_all%d" % g, align_bytes=64) for g in range(PASSES)]
+        xs_all = keep.tile([P, T], U8, name="xs_all", align_bytes=64)
+        corr_t = [keep.tile([P, D, V], F32, name="corr_t%d" % q, align_bytes=64) for q in range(D)]
+        raw = {}
+        width = {}
+        for q in range(D):
+            for (a, b) in LOADS[q]:
+                for g in range(PASSES):
+                    u = CHUNKS * q + a // P
+                    width[u] = b - a
+                    raw[(u, g)] = keep.tile([P, PACK, b - a], F32, name="raw", tag="raw%d_%d" % (u, g), align_bytes=64)
+
+        def load_x(g):
+            nc.sync.dma_start(out=x_all[g][:], in_=x_words[g].rearrange("p n t -> p (n t)").bitcast(I32))
+
+        def load_w(q, a, b, g):
+            part = weights[q][g * 512 : (g + 1) * 512, a:b]
+            nc.sync.dma_start(out=raw[(CHUNKS * q + a // P, g)][:], in_=part.rearrange("(p t) n -> p t n", t=PACK))
+
+        def load_corr(q):
+            nc.sync.dma_start(out=corr_t[q][:], in_=corr[D * q : D * q + D].rearrange("d p v -> p d v"))
+
+        nc.gpsimd.memset(xs_all[:].bitcast(I32), 0)
+        nc.sync.dma_start(offs_t[:], offs)
+        load_x(0)
+        for quad in range(4):
+            nc.scalar.dma_start(
+                out=xs_all[32 * quad : 32 * quad + 4 * PASSES, :].bitcast(I32),
+                in_=x_scales[:, 4 * quad : 4 * quad + 4, :].bitcast(I32),
+            )
+        load_x(1)
+        load_w(0, 0, 128, 0)
+        load_w(0, 0, 128, 1)
+        for q in range(D):
+            for n, (a, b) in enumerate(LOADS[q]):
+                if (q, a) != (0, 0):
+                    for g in range(PASSES):
+                        load_w(q, a, b, g)
+                if (q, n) == (0, 1):
+                    for d, pos in enumerate((pos1, pos2, pos3)):
+                        nc.sync.dma_start(pos_t[d][:], pos)
+                if n == (1 if q == 0 else 0):
+                    load_corr(q)
+
+        ident_raw = keep.tile([P, P], F32, name="ident_raw")
+        make_identity(nc, ident_raw[:])
+        ident = keep.tile([P, P], F32, name="ident")
+        nc.scalar.activation(out=ident[:], in_=ident_raw[:], func=RELU)
+
+        x_codes = [keep.tile([P, S], I32, name="x_codes%d" % g, align_bytes=64) for g in range(PASSES)]
+        x_planes = keep.tile([P, S], U8, name="x_planes", align_bytes=64)
+        nc.vector.tensor_copy(x_planes[:], xs_all[:].indirect(offs_t[:]))
+        nc.vector.tensor_copy(x_codes[0][:].bitcast(U32), x_all[0][:].bitcast(U32).indirect(offs_t[:]))
+        nc.vector.tensor_copy(x_codes[1][:].bitcast(U32), x_all[1][:].bitcast(U32).indirect(offs_t[:]))
+
+        LAST = CHUNKS - 1
+        acc_main = [banks.tile([P, LAST * P], F32, name="acc_main%d" % h, tag="main%d" % h) for h in range(HALVES)]
+        acc_last = [banks.tile([P, P], F32, name="acc_last%d" % h) for h in range(HALVES)]
+        summed = [keep.tile([P, PACK, P], F32, name="summed%d" % h, align_bytes=64) for h in range(HALVES)]
+
+        units = [(q, c) for q in range(D) for c in range(CHUNKS)]
+        rounded = {}
+        codes = {}
+        ybank = {}
+        y = {}
+
+        def cast(u, g):
+            if g == 0:
+                rounded[u] = ring.tile([P, PASSES, width[u], PACK], BF16, name="rounded", align_bytes=64)
+            nc.scalar.copy(
+                out=rounded[u][:, g].rearrange("p (c i) t -> p c t i", i=4),
+                in_=raw[(u, g)][:].rearrange("p t (c i) -> p c t i", i=4),
+            )
+
+        def quantise(u, g0, g1):
+            if g0 == 0:
+                w_codes = ring.tile([P, PASSES * width[u]], I32, name="w_codes", align_bytes=64)
+                w_planes = ring.tile([P, PASSES * width[u]], U8, name="w_planes", align_bytes=64)
+                codes[u] = (w_codes, w_planes)
+            w_codes, w_planes = codes[u]
+            a, b = g0 * width[u], g1 * width[u]
+            flat = rounded[u][:].rearrange("p g c t -> p (g c t)")
+            nc.vector.quantize_mx(out=w_codes[:, a:b].bitcast(FP8X4), scales=w_planes[:, a:b], in_=flat[:, PACK * a : PACK * b])
+
+        def multiply(u):
+            u0 = max(v for v in width if v <= u)
+            w_codes, w_planes = codes[u0]
+            ybank[u] = ybanks.tile([P, S], F32, name="ybank")
+            for g in range(PASSES):
+                c0 = g * width[u0] + (u - u0) * P
+                cols = slice(c0, c0 + P)
+                nc.tensor.matmul_mx(
+                    out=ybank[u][:],
+                    lhsT=w_codes[:, cols].bitcast(FP8X4),
+                    lhsT_scale=w_planes[:, cols],
+                    rhs=x_codes[g][:].bitcast(FP8X4),
+                    rhs_scale=x_planes[4 * g : P, :],
+                    start=(g == 0),
+                    stop=(g == PASSES - 1),
+                )
+
+        def unload(u):
+            y[u] = rows.tile([P, S], F32, name="y", align_bytes=64)
+            if u == 0:
+                nc.vector.tensor_copy(out=y[u][:], in_=ybank[u][:])
+            else:
+                nc.scalar.copy(out=y[u][:], in_=ybank[u][:])
+
+        def add_up(u, d, h, block):
+            q, c = units[u]
+            if c == LAST:
+                target = acc_last[h][:]
+                first, final = (q, d) == (0, 0), (q, d) == (D - 1, D - 1)
+            else:
+                target = acc_main[h][:, c * P : (c + 1) * P]
+                first, final = (q, c, d) == (0, 0, 0), (q, c, d) == (D - 1, LAST - 1, D - 1)
+            nc.tensor.matmul(out=target, lhsT=block, rhs=ident[:], is_transpose=True, start=first, stop=final)
+
+        def neighbour(u, d):
+            q, c = units[u]
+            if (u, d) in BEHIND:
+                prod = keep.tile([P, V], F32, name="prod_held", tag="raw%d_%d" % BEHIND[(u, d)], align_bytes=64)
+            else:
+                prod = prods.tile([P, V], F32, name="prod", align_bytes=64)
+            nc.vector.tensor_tensor(prod[:], y[u][:].indirect(pos_t[d][:]), corr_t[q][:, d, :], MULT)
+            for h in range(HALVES):
+                add_up(u, d, h, prod[:, h * P : (h + 1) * P])
+
+        def last_neighbours(u, h):
+            q, c = units[u]
+            for d in range(D):
+                prod = prods.tile([P, P], F32, name="prod", align_bytes=64)
+                nc.vector.tensor_tensor(
+                    prod[:], y[u][:].indirect(pos_t[d][:, 8 * h : 8 * h + 8]), corr_t[q][:, d, h * P : (h + 1) * P], MULT
+                )
+                add_up(u, d, h, prod[:])
+
+        def prepare(u, g):
+            if width[u] == P and u > 0:
+                cast(u, 0)
+                cast(u, 1)
+                quantise(u, 0, 2)
+            else:
+                cast(u, g)
+                quantise(u, g, g + 1)
+            if g == PASSES - 1:
+                for v in range(u, u + width[u] // P):
+                    multiply(v)
+
+        prepare(0, 0)
+        prepare(0, 1)
+        unload(0)
+        for u in range(len(units) - 1):
+            for d in range(D):
+                if (u, d) in BEHIND:
+                    prepare(*BEHIND[(u, d)])
+                neighbour(u, d)
+            unload(u + 1)
+        for h in range(HALVES):
+            nc.scalar.activation(
+                out=summed[h][:, :, 0 : LAST * 32], in_=acc_main[h][:].rearrange("v (p t) -> v t p", t=PACK), func=RELU
+            )
+        for h in range(HALVES):
+            last_neighbours(len(units) - 1, h)
+
+        out_words = keep.tile([P, V], I32, name="out_words", align_bytes=64)
+        out_planes = keep.tile([P, V], U8, name="out_planes", align_bytes=64)
+        out_rows = out_0.rearrange("(p t) v -> p t v", t=PACK)
+        for h in range(HALVES):
+            cols = slice(h * P, (h + 1) * P)
+            dealt = acc_last[h][:].rearrange("v (p t) -> v t p", t=PACK)
+            if h == 0:
+                nc.scalar.activation(out=summed[h][:, :, LAST * 32 : P], in_=dealt, func=RELU)
+            else:
+                nc.vector.tensor_scalar_max(summed[h][:, :, LAST * 32 : P], dealt, 0.0)
+            result = keep.tile([P, PACK, P], F32, name="result%d" % h, align_bytes=64)
+            result_bf = keep.tile([P, P, PACK], BF16, name="result_bf%d" % h, align_bytes=64)
+            if h == 0:
+                turned = banks.tile([P, PACK, P], F32, name="turned", tag="main0")
+                for t in range(PACK):
+                    nc.tensor.transpose(turned[:, t, :], summed[h][:, t, :], ident[:])
+                nc.scalar.copy(out=result[:], in_=turned[:])
+                nc.vector.tensor_copy(
+                    out=result_bf[:].rearrange("p (c i) t -> p c t i", i=4), in_=result[:].rearrange("p t (c i) -> p c t i", i=4)
+                )
+            else:
+                pairs = [ybanks.tile([P, 2, P], F32, name="ybank") for j in range(2)]
+                for t in range(PACK):
+                    nc.tensor.transpose(pairs[t // 2][:, t % 2, :], summed[h][:, t, :], ident[:])
+                for j in range(2):
+                    nc.vector.tensor_copy(out=result_bf[:, :, 2 * j : 2 * j + 2], in_=pairs[j][:].rearrange("p t c -> p c t"))
+                    nc.scalar.copy(out=result[:, 2 - 2 * j : 4 - 2 * j, :], in_=pairs[1 - j][:])
+            nc.sync.dma_start(out=out_rows[:, :, cols], in_=result[:])
+            nc.vector.quantize_mx(
+                out=out_words[:, cols].bitcast(FP8X4), scales=out_planes[:, cols], in_=result_bf[:].rearrange("p c t -> p (c t)")
+            )
+        nc.sync.dma_start(out=out_1[0].rearrange("p c r -> p (c r)").bitcast(I32), in_=out_words[:])
+        for quad in range(4):
+            queue = nc.scalar if quad % 2 else nc.sync
+            queue.dma_start(
+                out=out_2[0][4 * quad : 4 * quad + 4, :].bitcast(I32), in_=out_planes[32 * quad : 32 * quad + 4, :].bitcast(I32)
+            )

@@ -21,9 +21,8 @@ CHUNKS = N // P
 HALVES = V // P
 FLOPS = 2 * K * N * S * D
 
-LOADS = [[(0, 128), (128, 256), (256, 384), (384, 512)], [(0, 256), (256, 512)], [(0, 256), (256, 512)]]
-BEHIND = {(0, 0): (1, 1), (1, 0): (2, 1), (1, 2): (3, 1), (2, 1): (4, 0), (2, 2): (4, 1), (4, 1): (6, 0), (4, 2): (6, 1),
-          (6, 1): (8, 0), (6, 2): (8, 1), (8, 1): (10, 0), (8, 2): (10, 1)}
+UNITS = D * CHUNKS
+DEEPER_FROM = 5
 
 
 def tile_picked_zkp_three_po_kernel(tc, x_words, x_scales, w1, w2, w3, corr, offs, pos1, pos2, pos3, out_0, out_1, out_2):
@@ -32,9 +31,8 @@ def tile_picked_zkp_three_po_kernel(tc, x_words, x_scales, w1, w2, w3, corr, off
     with ExitStack() as ctx:
         lists = ctx.enter_context(tc.tile_pool(name="lists", bufs=1))
         keep = ctx.enter_context(tc.tile_pool(name="keep", bufs=1))
-        ring = ctx.enter_context(tc.tile_pool(name="ring", bufs=3))
-        rows = ctx.enter_context(tc.tile_pool(name="rows", bufs=4))
-        prods = ctx.enter_context(tc.tile_pool(name="prods", bufs=6))
+        ring = ctx.enter_context(tc.tile_pool(name="ring", bufs=4))
+        prods = ctx.enter_context(tc.tile_pool(name="prods", bufs=8))
         ybanks = ctx.enter_context(tc.psum_pool(name="ybanks", bufs=4))
         banks = ctx.enter_context(tc.psum_pool(name="banks", bufs=1))
 
@@ -44,20 +42,17 @@ def tile_picked_zkp_three_po_kernel(tc, x_words, x_scales, w1, w2, w3, corr, off
         xs_all = keep.tile([P, T], U8, name="xs_all", align_bytes=64)
         corr_t = [keep.tile([P, D, V], F32, name="corr_t%d" % q, align_bytes=64) for q in range(D)]
         raw = {}
-        width = {}
-        for q in range(D):
-            for (a, b) in LOADS[q]:
-                for g in range(PASSES):
-                    u = CHUNKS * q + a // P
-                    width[u] = b - a
-                    raw[(u, g)] = keep.tile([P, PACK, b - a], F32, name="raw", tag="raw%d_%d" % (u, g), align_bytes=64)
 
         def load_x(g):
             nc.sync.dma_start(out=x_all[g][:], in_=x_words[g].rearrange("p n t -> p (n t)").bitcast(I32))
 
-        def load_w(q, a, b, g):
-            part = weights[q][g * 512 : (g + 1) * 512, a:b]
-            nc.sync.dma_start(out=raw[(CHUNKS * q + a // P, g)][:], in_=part.rearrange("(p t) n -> p t n", t=PACK))
+        def load_w(u, g, count):
+            q, c = divmod(u, CHUNKS)
+            tile = keep.tile([P, PACK, count * P], F32, name="raw", tag="raw%d_%d" % (u, g), align_bytes=64)
+            part = weights[q][g * 512 : (g + 1) * 512, c * P : (c + count) * P]
+            nc.sync.dma_start(out=tile[:], in_=part.rearrange("(p t) n -> p t n", t=PACK))
+            for j in range(count):
+                raw[(u + j, g)] = tile[:, :, j * P : (j + 1) * P]
 
         def load_corr(q):
             nc.sync.dma_start(out=corr_t[q][:], in_=corr[D * q : D * q + D].rearrange("d p v -> p d v"))
@@ -66,34 +61,36 @@ def tile_picked_zkp_three_po_kernel(tc, x_words, x_scales, w1, w2, w3, corr, off
         nc.sync.dma_start(offs_t[:], offs)
         load_x(0)
         for quad in range(4):
-            nc.scalar.dma_start(
+            nc.sync.dma_start(
                 out=xs_all[32 * quad : 32 * quad + 4 * PASSES, :].bitcast(I32),
                 in_=x_scales[:, 4 * quad : 4 * quad + 4, :].bitcast(I32),
             )
+        load_w(0, 0, 1)
+        load_w(0, 1, 1)
         load_x(1)
-        load_w(0, 0, 128, 0)
-        load_w(0, 0, 128, 1)
-        for q in range(D):
-            for n, (a, b) in enumerate(LOADS[q]):
-                if (q, a) != (0, 0):
-                    for g in range(PASSES):
-                        load_w(q, a, b, g)
-                if (q, n) == (0, 1):
-                    for d, pos in enumerate((pos1, pos2, pos3)):
-                        nc.sync.dma_start(pos_t[d][:], pos)
-                if n == (1 if q == 0 else 0):
-                    load_corr(q)
+        load_w(1, 0, 1)
+        load_w(1, 1, 1)
+        for d, pos in enumerate((pos1, pos2, pos3)):
+            nc.sync.dma_start(pos_t[d][:], pos)
+        load_corr(0)
+        for u in range(2, UNITS):
+            if u < CHUNKS:
+                load_w(u, 0, 1)
+            elif u % 2 == 0:
+                load_w(u, 0, 2)
+            load_w(u, 1, 1)
+            if u > CHUNKS and u % CHUNKS == 1:
+                load_corr(u // CHUNKS)
 
         ident_raw = keep.tile([P, P], F32, name="ident_raw")
         make_identity(nc, ident_raw[:])
         ident = keep.tile([P, P], F32, name="ident")
         nc.scalar.activation(out=ident[:], in_=ident_raw[:], func=RELU)
 
-        x_codes = [keep.tile([P, S], I32, name="x_codes%d" % g, align_bytes=64) for g in range(PASSES)]
+        x_codes = [keep.tile([P, S], I32, name="x_codes0", align_bytes=64)]
         x_planes = keep.tile([P, S], U8, name="x_planes", align_bytes=64)
-        nc.vector.tensor_copy(x_planes[:], xs_all[:].indirect(offs_t[:]))
         nc.vector.tensor_copy(x_codes[0][:].bitcast(U32), x_all[0][:].bitcast(U32).indirect(offs_t[:]))
-        nc.vector.tensor_copy(x_codes[1][:].bitcast(U32), x_all[1][:].bitcast(U32).indirect(offs_t[:]))
+        nc.vector.tensor_copy(x_planes[:], xs_all[:].indirect(offs_t[:]))
 
         LAST = CHUNKS - 1
         acc_main = [banks.tile([P, LAST * P], F32, name="acc_main%d" % h, tag="main%d" % h) for h in range(HALVES)]
@@ -108,29 +105,27 @@ def tile_picked_zkp_three_po_kernel(tc, x_words, x_scales, w1, w2, w3, corr, off
 
         def cast(u, g):
             if g == 0:
-                rounded[u] = ring.tile([P, PASSES, width[u], PACK], BF16, name="rounded", align_bytes=64)
+                rounded[u] = keep.tile([P, PASSES, P, PACK], BF16, name="rounded", tag="rounded%d" % u, align_bytes=64)
             nc.scalar.copy(
                 out=rounded[u][:, g].rearrange("p (c i) t -> p c t i", i=4),
-                in_=raw[(u, g)][:].rearrange("p t (c i) -> p c t i", i=4),
+                in_=raw[(u, g)].rearrange("p t (c i) -> p c t i", i=4),
             )
 
         def quantise(u, g0, g1):
             if g0 == 0:
-                w_codes = ring.tile([P, PASSES * width[u]], I32, name="w_codes", align_bytes=64)
-                w_planes = ring.tile([P, PASSES * width[u]], U8, name="w_planes", align_bytes=64)
+                w_codes = ring.tile([P, PASSES * P], I32, name="w_codes", align_bytes=64)
+                w_planes = ring.tile([P, PASSES * P], U8, name="w_planes", align_bytes=64)
                 codes[u] = (w_codes, w_planes)
             w_codes, w_planes = codes[u]
-            a, b = g0 * width[u], g1 * width[u]
-            flat = rounded[u][:].rearrange("p g c t -> p (g c t)")
-            nc.vector.quantize_mx(out=w_codes[:, a:b].bitcast(FP8X4), scales=w_planes[:, a:b], in_=flat[:, PACK * a : PACK * b])
+            a, b = g0 * P, g1 * P
+            source = rounded[u][:].rearrange("p g c t -> p (g c t)")[:, PACK * a : PACK * b]
+            nc.vector.quantize_mx(out=w_codes[:, a:b].bitcast(FP8X4), scales=w_planes[:, a:b], in_=source)
 
         def multiply(u):
-            u0 = max(v for v in width if v <= u)
-            w_codes, w_planes = codes[u0]
+            w_codes, w_planes = codes[u]
             ybank[u] = ybanks.tile([P, S], F32, name="ybank")
             for g in range(PASSES):
-                c0 = g * width[u0] + (u - u0) * P
-                cols = slice(c0, c0 + P)
+                cols = slice(g * P, (g + 1) * P)
                 nc.tensor.matmul_mx(
                     out=ybank[u][:],
                     lhsT=w_codes[:, cols].bitcast(FP8X4),
@@ -141,12 +136,13 @@ def tile_picked_zkp_three_po_kernel(tc, x_words, x_scales, w1, w2, w3, corr, off
                     stop=(g == PASSES - 1),
                 )
 
+        def lead(u):
+            return 2 if u >= DEEPER_FROM else 1
+
         def unload(u):
-            y[u] = rows.tile([P, S], F32, name="y", align_bytes=64)
-            if u == 0:
-                nc.vector.tensor_copy(out=y[u][:], in_=ybank[u][:])
-            else:
-                nc.scalar.copy(out=y[u][:], in_=ybank[u][:])
+            ahead = u + lead(u)
+            y[u] = keep.tile([P, S], F32, name="y", tag="raw%d_1" % ahead if ahead < UNITS else "y%d" % u, align_bytes=64)
+            nc.scalar.copy(out=y[u][:], in_=ybank[u][:])
 
         def add_up(u, d, h, block):
             q, c = units[u]
@@ -160,11 +156,11 @@ def tile_picked_zkp_three_po_kernel(tc, x_words, x_scales, w1, w2, w3, corr, off
 
         def neighbour(u, d):
             q, c = units[u]
-            if (u, d) in BEHIND:
-                prod = keep.tile([P, V], F32, name="prod_held", tag="raw%d_%d" % BEHIND[(u, d)], align_bytes=64)
+            if u == 0:
+                prod = first_prods[:, d, :]
             else:
-                prod = prods.tile([P, V], F32, name="prod", align_bytes=64)
-            nc.vector.tensor_tensor(prod[:], y[u][:].indirect(pos_t[d][:]), corr_t[q][:, d, :], MULT)
+                prod = prods.tile([P, V], F32, name="prod", align_bytes=64)[:]
+            nc.vector.tensor_tensor(prod, y[u][:].indirect(pos_t[d][:]), corr_t[q][:, d, :], MULT)
             for h in range(HALVES):
                 add_up(u, d, h, prod[:, h * P : (h + 1) * P])
 
@@ -177,27 +173,49 @@ def tile_picked_zkp_three_po_kernel(tc, x_words, x_scales, w1, w2, w3, corr, off
                 )
                 add_up(u, d, h, prod[:])
 
-        def prepare(u, g):
-            if width[u] == P and u > 0:
-                cast(u, 0)
-                cast(u, 1)
-                quantise(u, 0, 2)
-            else:
+        for g in range(PASSES):
+            cast(0, g)
+            quantise(0, g, g + 1)
+        w_codes, w_planes = codes[0]
+        x_codes.append(keep.tile([P, S], I32, name="x_codes1", tag="raw0_1", align_bytes=64))
+        y[0] = keep.tile([P, S], F32, name="y", align_bytes=64)
+        first = [ybanks.tile([P, S // 2], F32, name="ybank") for j in range(2)]
+        for g in range(PASSES):
+            for j in range(2):
+                part = slice(j * S // 2, (j + 1) * S // 2)
+                if g == PASSES - 1:
+                    nc.vector.tensor_copy(
+                        x_codes[g][:, part].bitcast(U32), x_all[g][:].bitcast(U32).indirect(offs_t[:, 16 * j : 16 * j + 16])
+                    )
+                nc.tensor.matmul_mx(
+                    out=first[j][:],
+                    lhsT=w_codes[:, g * P : (g + 1) * P].bitcast(FP8X4),
+                    lhsT_scale=w_planes[:, g * P : (g + 1) * P],
+                    rhs=x_codes[g][:, part].bitcast(FP8X4),
+                    rhs_scale=x_planes[4 * g : P, part],
+                    start=(g == 0),
+                    stop=(g == PASSES - 1),
+                )
+        nc.vector.tensor_copy(out=y[0][:, 0 : S // 2], in_=first[0][:])
+        nc.vector.tensor_copy(out=y[0][:, S // 2 : S], in_=first[1][:])
+        def prepare(u):
+            for g in range(PASSES):
                 cast(u, g)
-                quantise(u, g, g + 1)
-            if g == PASSES - 1:
-                for v in range(u, u + width[u] // P):
-                    multiply(v)
+            quantise(u, 0, PASSES)
+            multiply(u)
 
-        prepare(0, 0)
-        prepare(0, 1)
-        unload(0)
-        for u in range(len(units) - 1):
-            for d in range(D):
-                if (u, d) in BEHIND:
-                    prepare(*BEHIND[(u, d)])
-                neighbour(u, d)
-            unload(u + 1)
+        prepare(1)
+        prepared = 1
+        first_prods = keep.tile([P, D, V], F32, name="first_prods", tag="rounded1", align_bytes=64)
+        for u in range(UNITS):
+            if u > 0:
+                while prepared < min(u + lead(u), UNITS - 1):
+                    prepared = prepared + 1
+                    prepare(prepared)
+                unload(u)
+            if u < UNITS - 1:
+                for d in range(D):
+                    neighbour(u, d)
         for h in range(HALVES):
             nc.scalar.activation(
                 out=summed[h][:, :, 0 : LAST * 32], in_=acc_main[h][:].rearrange("v (p t) -> v t p", t=PACK), func=RELU
@@ -236,7 +254,7 @@ def tile_picked_zkp_three_po_kernel(tc, x_words, x_scales, w1, w2, w3, corr, off
             nc.vector.quantize_mx(
                 out=out_words[:, cols].bitcast(FP8X4), scales=out_planes[:, cols], in_=result_bf[:].rearrange("p c t -> p (c t)")
             )
-        nc.sync.dma_start(out=out_1[0].rearrange("p c r -> p (c r)").bitcast(I32), in_=out_words[:])
+            nc.sync.dma_start(out=out_1[0].rearrange("p c r -> p (c r)").bitcast(I32)[:, cols], in_=out_words[:, cols])
         for quad in range(4):
             queue = nc.scalar if quad % 2 else nc.sync
             queue.dma_start(

@@ -78,7 +78,10 @@ def tile_picked_zkp_three_po_kernel(tc, x_words, x_scales, w1, w2, w3, corr, off
                 load_w(u, 0, 1)
             elif u % 2 == 0:
                 load_w(u, 0, 2)
-            load_w(u, 1, 1)
+            if u <= DEEPER_FROM:
+                load_w(u, 1, 1)
+            elif u % 2 == 0:
+                load_w(u, 1, 2)
             if u > CHUNKS and u % CHUNKS == 1:
                 load_corr(u // CHUNKS)
 
@@ -136,12 +139,14 @@ def tile_picked_zkp_three_po_kernel(tc, x_words, x_scales, w1, w2, w3, corr, off
                     stop=(g == PASSES - 1),
                 )
 
-        def lead(u):
-            return 2 if u >= DEEPER_FROM else 1
-
         def unload(u):
-            ahead = u + lead(u)
-            y[u] = keep.tile([P, S], F32, name="y", tag="raw%d_1" % ahead if ahead < UNITS else "y%d" % u, align_bytes=64)
+            if u >= UNITS - 2:
+                tag = "y%d" % u
+            elif u > DEEPER_FROM and u % 2 == 0:
+                tag = "raw%d_0" % (u + 2)
+            else:
+                tag = "raw%d_1" % (u + 1)
+            y[u] = keep.tile([P, S], F32, name="y", tag=tag, align_bytes=64)
             nc.scalar.copy(out=y[u][:], in_=ybank[u][:])
 
         def add_up(u, d, h, block):
@@ -198,20 +203,29 @@ def tile_picked_zkp_three_po_kernel(tc, x_words, x_scales, w1, w2, w3, corr, off
                 )
         nc.vector.tensor_copy(out=y[0][:, 0 : S // 2], in_=first[0][:])
         nc.vector.tensor_copy(out=y[0][:, S // 2 : S], in_=first[1][:])
-        def prepare(u):
-            for g in range(PASSES):
-                cast(u, g)
+        def finish(u):
+            cast(u, 1)
             quantise(u, 0, PASSES)
             multiply(u)
 
-        prepare(1)
-        prepared = 1
+        cast(1, 0)
+        finish(1)
         first_prods = keep.tile([P, D, V], F32, name="first_prods", tag="rounded1", align_bytes=64)
         for u in range(UNITS):
+            if 0 < u < DEEPER_FROM:
+                cast(u + 1, 0)
+                finish(u + 1)
+            elif DEEPER_FROM <= u < UNITS - 2:
+                if u == DEEPER_FROM:
+                    cast(u + 1, 0)
+                    cast(u + 2, 0)
+                if u % 2 == 0:
+                    cast(u + 2, 0)
+                    cast(u + 3, 0)
+                else:
+                    finish(u + 1)
+                    finish(u + 2)
             if u > 0:
-                while prepared < min(u + lead(u), UNITS - 1):
-                    prepared = prepared + 1
-                    prepare(prepared)
                 unload(u)
             if u < UNITS - 1:
                 for d in range(D):
@@ -225,36 +239,30 @@ def tile_picked_zkp_three_po_kernel(tc, x_words, x_scales, w1, w2, w3, corr, off
 
         out_words = keep.tile([P, V], I32, name="out_words", align_bytes=64)
         out_planes = keep.tile([P, V], U8, name="out_planes", align_bytes=64)
+        result_bf = keep.tile([P, V, PACK], BF16, name="result_bf", align_bytes=64)
         out_rows = out_0.rearrange("(p t) v -> p t v", t=PACK)
-        for h in range(HALVES):
-            cols = slice(h * P, (h + 1) * P)
-            dealt = acc_last[h][:].rearrange("v (p t) -> v t p", t=PACK)
-            if h == 0:
-                nc.scalar.activation(out=summed[h][:, :, LAST * 32 : P], in_=dealt, func=RELU)
-            else:
-                nc.vector.tensor_scalar_max(summed[h][:, :, LAST * 32 : P], dealt, 0.0)
-            result = keep.tile([P, PACK, P], F32, name="result%d" % h, align_bytes=64)
-            result_bf = keep.tile([P, P, PACK], BF16, name="result_bf%d" % h, align_bytes=64)
-            if h == 0:
-                turned = banks.tile([P, PACK, P], F32, name="turned", tag="main0")
-                for t in range(PACK):
-                    nc.tensor.transpose(turned[:, t, :], summed[h][:, t, :], ident[:])
-                nc.scalar.copy(out=result[:], in_=turned[:])
-                nc.vector.tensor_copy(
-                    out=result_bf[:].rearrange("p (c i) t -> p c t i", i=4), in_=result[:].rearrange("p t (c i) -> p c t i", i=4)
-                )
-            else:
-                pairs = [ybanks.tile([P, 2, P], F32, name="ybank") for j in range(2)]
-                for t in range(PACK):
-                    nc.tensor.transpose(pairs[t // 2][:, t % 2, :], summed[h][:, t, :], ident[:])
-                for j in range(2):
-                    nc.vector.tensor_copy(out=result_bf[:, :, 2 * j : 2 * j + 2], in_=pairs[j][:].rearrange("p t c -> p c t"))
-                    nc.scalar.copy(out=result[:, 2 - 2 * j : 4 - 2 * j, :], in_=pairs[1 - j][:])
-            nc.sync.dma_start(out=out_rows[:, :, cols], in_=result[:])
-            nc.vector.quantize_mx(
-                out=out_words[:, cols].bitcast(FP8X4), scales=out_planes[:, cols], in_=result_bf[:].rearrange("p c t -> p (c t)")
-            )
-            nc.sync.dma_start(out=out_1[0].rearrange("p c r -> p (c r)").bitcast(I32)[:, cols], in_=out_words[:, cols])
+        result = [keep.tile([P, PACK, P], F32, name="result%d" % h, align_bytes=64) for h in range(HALVES)]
+        dealt = [acc_last[h][:].rearrange("v (p t) -> v t p", t=PACK) for h in range(HALVES)]
+        nc.scalar.activation(out=summed[0][:, :, LAST * 32 : P], in_=dealt[0], func=RELU)
+        turned = banks.tile([P, PACK, P], F32, name="turned", tag="main0")
+        for t in range(PACK):
+            nc.tensor.transpose(turned[:, t, :], summed[0][:, t, :], ident[:])
+        nc.scalar.copy(out=result[0][:], in_=turned[:])
+        nc.sync.dma_start(out=out_rows[:, :, 0:P], in_=result[0][:])
+        nc.vector.tensor_scalar_max(summed[1][:, :, LAST * 32 : P], dealt[1], 0.0)
+        pairs = [ybanks.tile([P, 2, P], F32, name="ybank") for j in range(2)]
+        for t in range(PACK):
+            nc.tensor.transpose(pairs[t // 2][:, t % 2, :], summed[1][:, t, :], ident[:])
+        nc.vector.tensor_copy(out=result_bf[:, P:V, 0:2], in_=pairs[0][:].rearrange("p t c -> p c t"))
+        nc.scalar.copy(out=result[1][:, 2:4, :], in_=pairs[1][:])
+        nc.vector.tensor_copy(
+            out=result_bf[:, 0:P, :].rearrange("p (c i) t -> p c t i", i=4), in_=result[0][:].rearrange("p t (c i) -> p c t i", i=4)
+        )
+        nc.scalar.copy(out=result[1][:, 0:2, :], in_=pairs[0][:])
+        nc.vector.tensor_copy(out=result_bf[:, P:V, 2:4], in_=pairs[1][:].rearrange("p t c -> p c t"))
+        nc.sync.dma_start(out=out_rows[:, :, P:V], in_=result[1][:])
+        nc.vector.quantize_mx(out=out_words[:].bitcast(FP8X4), scales=out_planes[:], in_=result_bf[:].rearrange("p c t -> p (c t)"))
+        nc.scalar.dma_start(out=out_1[0].rearrange("p c r -> p (c r)").bitcast(I32), in_=out_words[:])
         for quad in range(4):
             queue = nc.scalar if quad % 2 else nc.sync
             queue.dma_start(

@@ -12,6 +12,7 @@ U8 = mybir.dt.uint8
 FP8X4 = mybir.dt.float8_e4m3fn_x4
 RELU = mybir.ActivationFunctionType.Relu
 MULT = mybir.AluOpType.mult
+ADD = mybir.AluOpType.add
 
 K, T, S, D, V, N = 1024, 1024, 512, 3, 256, 512
 P = 128
@@ -22,7 +23,7 @@ HALVES = V // P
 FLOPS = 2 * K * N * S * D
 
 UNITS = D * CHUNKS
-DEEPER_FROM = 5
+DEALT_FROM = (D - 1) * CHUNKS
 
 
 def tile_picked_zkp_three_po_kernel(tc, x_words, x_scales, w1, w2, w3, corr, offs, pos1, pos2, pos3, out_0, out_1, out_2):
@@ -31,6 +32,7 @@ def tile_picked_zkp_three_po_kernel(tc, x_words, x_scales, w1, w2, w3, corr, off
     with ExitStack() as ctx:
         lists = ctx.enter_context(tc.tile_pool(name="lists", bufs=1))
         keep = ctx.enter_context(tc.tile_pool(name="keep", bufs=1))
+        placed = ctx.enter_context(tc.tile_pool(name="placed", bufs=1))
         ring = ctx.enter_context(tc.tile_pool(name="ring", bufs=4))
         prods = ctx.enter_context(tc.tile_pool(name="prods", bufs=8))
         ybanks = ctx.enter_context(tc.psum_pool(name="ybanks", bufs=4))
@@ -54,6 +56,12 @@ def tile_picked_zkp_three_po_kernel(tc, x_words, x_scales, w1, w2, w3, corr, off
             for j in range(count):
                 raw[(u + j, g)] = tile[:, :, j * P : (j + 1) * P]
 
+        whole = []
+
+        def load_whole(g):
+            whole.append(keep.tile([P, PACK, N], F32, name="whole%d" % g, align_bytes=64))
+            nc.sync.dma_start(out=whole[g][:], in_=weights[D - 1][g * 512 : (g + 1) * 512, :].rearrange("(p t) n -> p t n", t=PACK))
+
         def load_corr(q):
             nc.sync.dma_start(out=corr_t[q][:], in_=corr[D * q : D * q + D].rearrange("d p v -> p d v"))
 
@@ -73,17 +81,18 @@ def tile_picked_zkp_three_po_kernel(tc, x_words, x_scales, w1, w2, w3, corr, off
         for d, pos in enumerate((pos1, pos2, pos3)):
             nc.sync.dma_start(pos_t[d][:], pos)
         load_corr(0)
-        for u in range(2, UNITS):
+        for u in range(2, DEALT_FROM):
             if u < CHUNKS:
                 load_w(u, 0, 1)
             elif u % 2 == 0:
                 load_w(u, 0, 2)
-            if u <= DEEPER_FROM:
-                load_w(u, 1, 1)
-            elif u % 2 == 0:
-                load_w(u, 1, 2)
+            if u == DEALT_FROM - 1:
+                load_whole(0)
+            load_w(u, 1, 1)
             if u > CHUNKS and u % CHUNKS == 1:
                 load_corr(u // CHUNKS)
+        load_whole(1)
+        load_corr(D - 1)
 
         ident_raw = keep.tile([P, P], F32, name="ident_raw")
         make_identity(nc, ident_raw[:])
@@ -95,12 +104,8 @@ def tile_picked_zkp_three_po_kernel(tc, x_words, x_scales, w1, w2, w3, corr, off
         nc.vector.tensor_copy(x_codes[0][:].bitcast(U32), x_all[0][:].bitcast(U32).indirect(offs_t[:]))
         nc.vector.tensor_copy(x_planes[:], xs_all[:].indirect(offs_t[:]))
 
-        LAST = CHUNKS - 1
-        acc_main = [banks.tile([P, LAST * P], F32, name="acc_main%d" % h, tag="main%d" % h) for h in range(HALVES)]
-        acc_last = [banks.tile([P, P], F32, name="acc_last%d" % h) for h in range(HALVES)]
-        summed = [keep.tile([P, PACK, P], F32, name="summed%d" % h, align_bytes=64) for h in range(HALVES)]
+        acc = [banks.tile([P, N], F32, name="acc%d" % h, tag="acc%d" % h) for h in range(HALVES)]
 
-        units = [(q, c) for q in range(D) for c in range(CHUNKS)]
         rounded = {}
         codes = {}
         ybank = {}
@@ -108,10 +113,22 @@ def tile_picked_zkp_three_po_kernel(tc, x_words, x_scales, w1, w2, w3, corr, off
 
         def cast(u, g):
             if g == 0:
-                rounded[u] = keep.tile([P, PASSES, P, PACK], BF16, name="rounded", tag="rounded%d" % u, align_bytes=64)
+                rounded[u] = keep.tile([P, PASSES, P, PACK], BF16, name="rounded", tag="rounded%d" % u, align_bytes=64)[:]
             nc.scalar.copy(
                 out=rounded[u][:, g].rearrange("p (c i) t -> p c t i", i=4),
                 in_=raw[(u, g)].rearrange("p t (c i) -> p c t i", i=4),
+            )
+
+        def cast_dealt(u, g):
+            if g == 0:
+                start = 3072 if u == DEALT_FROM else 7104
+                both = placed.tile([P, 2, PASSES, P, PACK], BF16, name="rounded", tag="rounded%d" % u, align_bytes=64, offset=start)
+                rounded[(u, u + 1)] = both
+                rounded[u], rounded[u + 1] = both[:, 0], both[:, 1]
+            s = u - DEALT_FROM
+            nc.scalar.copy(
+                out=rounded[(u, u + 1)][:, :, g].rearrange("p s m t -> p m t s"),
+                in_=whole[g][:].rearrange("p t (m s) -> p m t s", s=PACK)[:, :, :, s : s + 2],
             )
 
         def quantise(u, g0, g1):
@@ -121,7 +138,7 @@ def tile_picked_zkp_three_po_kernel(tc, x_words, x_scales, w1, w2, w3, corr, off
                 codes[u] = (w_codes, w_planes)
             w_codes, w_planes = codes[u]
             a, b = g0 * P, g1 * P
-            source = rounded[u][:].rearrange("p g c t -> p (g c t)")[:, PACK * a : PACK * b]
+            source = rounded[u].rearrange("p g c t -> p (g c t)")[:, PACK * a : PACK * b]
             nc.vector.quantize_mx(out=w_codes[:, a:b].bitcast(FP8X4), scales=w_planes[:, a:b], in_=source)
 
         def multiply(u):
@@ -140,50 +157,42 @@ def tile_picked_zkp_three_po_kernel(tc, x_words, x_scales, w1, w2, w3, corr, off
                 )
 
         def unload(u):
-            if u >= UNITS - 2:
-                tag = "y%d" % u
-            elif u > DEEPER_FROM and u % 2 == 0:
-                tag = "raw%d_0" % (u + 2)
-            else:
+            if u < DEALT_FROM - 1:
                 tag = "raw%d_1" % (u + 1)
+            else:
+                tag = "y%d" % u
             y[u] = keep.tile([P, S], F32, name="y", tag=tag, align_bytes=64)
             nc.scalar.copy(out=y[u][:], in_=ybank[u][:])
 
-        def add_up(u, d, h, block):
-            q, c = units[u]
-            if c == LAST:
-                target = acc_last[h][:]
-                first, final = (q, d) == (0, 0), (q, d) == (D - 1, D - 1)
-            else:
-                target = acc_main[h][:, c * P : (c + 1) * P]
-                first, final = (q, c, d) == (0, 0, 0), (q, c, d) == (D - 1, LAST - 1, D - 1)
+        def turn(target, block, first, final):
             nc.tensor.matmul(out=target, lhsT=block, rhs=ident[:], is_transpose=True, start=first, stop=final)
 
+        def gather(prod, u, d, lo, hi):
+            nc.vector.tensor_tensor(prod, y[u][:].indirect(pos_t[d][:, lo // 16 : hi // 16]), corr_t[u // CHUNKS][:, d, lo:hi], MULT)
+
+        held = {}
+
         def neighbour(u, d):
-            q, c = units[u]
-            if u == 0:
-                prod = first_prods[:, d, :]
+            if u in held:
+                prod = held[u][:, d, :]
+            elif (u, d) == (DEALT_FROM - 2, 1):
+                prod = keep.tile([P, V], F32, name="prod", tag="y%d" % (u + 1), align_bytes=64)[:]
             else:
                 prod = prods.tile([P, V], F32, name="prod", align_bytes=64)[:]
-            nc.vector.tensor_tensor(prod, y[u][:].indirect(pos_t[d][:]), corr_t[q][:, d, :], MULT)
+            gather(prod, u, d, 0, V)
             for h in range(HALVES):
-                add_up(u, d, h, prod[:, h * P : (h + 1) * P])
-
-        def last_neighbours(u, h):
-            q, c = units[u]
-            for d in range(D):
-                prod = prods.tile([P, P], F32, name="prod", align_bytes=64)
-                nc.vector.tensor_tensor(
-                    prod[:], y[u][:].indirect(pos_t[d][:, 8 * h : 8 * h + 8]), corr_t[q][:, d, h * P : (h + 1) * P], MULT
-                )
-                add_up(u, d, h, prod[:])
+                if u < DEALT_FROM:
+                    c = u % CHUNKS
+                    target = acc[h][:, c * P : (c + 1) * P]
+                else:
+                    target = acc[h][:].rearrange("v (p t) -> v t p", t=PACK)[:, u - DEALT_FROM, :]
+                turn(target, prod[:, h * P : (h + 1) * P], (u, d) == (0, 0), (u, d) == (UNITS - 3, D - 1))
 
         for g in range(PASSES):
             cast(0, g)
             quantise(0, g, g + 1)
-        w_codes, w_planes = codes[0]
         x_codes.append(keep.tile([P, S], I32, name="x_codes1", tag="raw0_1", align_bytes=64))
-        y[0] = keep.tile([P, S], F32, name="y", align_bytes=64)
+        w_codes, w_planes = codes[0]
         first = [ybanks.tile([P, S // 2], F32, name="ybank") for j in range(2)]
         for g in range(PASSES):
             for j in range(2):
@@ -201,8 +210,6 @@ def tile_picked_zkp_three_po_kernel(tc, x_words, x_scales, w1, w2, w3, corr, off
                     start=(g == 0),
                     stop=(g == PASSES - 1),
                 )
-        nc.vector.tensor_copy(out=y[0][:, 0 : S // 2], in_=first[0][:])
-        nc.vector.tensor_copy(out=y[0][:, S // 2 : S], in_=first[1][:])
         def finish(u):
             cast(u, 1)
             quantise(u, 0, PASSES)
@@ -210,58 +217,92 @@ def tile_picked_zkp_three_po_kernel(tc, x_words, x_scales, w1, w2, w3, corr, off
 
         cast(1, 0)
         finish(1)
-        first_prods = keep.tile([P, D, V], F32, name="first_prods", tag="rounded1", align_bytes=64)
-        for u in range(UNITS):
-            if 0 < u < DEEPER_FROM:
+        y[0] = keep.tile([P, S], F32, name="y", tag="raw1_1", align_bytes=64)
+        nc.vector.tensor_copy(out=y[0][:, 0 : S // 2], in_=first[0][:])
+        nc.scalar.copy(out=y[0][:, S // 2 : S], in_=first[1][:])
+        for u in range(UNITS - 2):
+            if 0 < u < DEALT_FROM - 1:
                 cast(u + 1, 0)
+                if u == DEALT_FROM - 2:
+                    cast_dealt(u + 2, 0)
                 finish(u + 1)
-            elif DEEPER_FROM <= u < UNITS - 2:
-                if u == DEEPER_FROM:
-                    cast(u + 1, 0)
-                    cast(u + 2, 0)
-                if u % 2 == 0:
-                    cast(u + 2, 0)
-                    cast(u + 3, 0)
-                else:
-                    finish(u + 1)
-                    finish(u + 2)
+            elif u == DEALT_FROM:
+                cast_dealt(u + 2, 0)
+            elif u == DEALT_FROM - 1 or u == DEALT_FROM + 1:
+                cast_dealt(u + 1, 1)
+                for j in range(1, 3):
+                    quantise(u + j, 0, PASSES)
+                    multiply(u + j)
+                if u < DEALT_FROM:
+                    held[u] = placed.tile([P, D, V], F32, name="held_prods", align_bytes=64, offset=64)
             if u > 0:
                 unload(u)
-            if u < UNITS - 1:
-                for d in range(D):
-                    neighbour(u, d)
+            for d in range(D):
+                neighbour(u, d)
+
+        pair = (UNITS - 2, UNITS - 1)
+        unload(pair[0])
+        unload(pair[1])
+        mid_first = banks.tile([P, HALVES, P], F32, name="mid_first")
+        mid_last = [ybanks.tile([P, P], F32, name="ybank") for h in range(HALVES)]
+        for d in range(D - 1):
+            prod = prods.tile([P, V], F32, name="prod", align_bytes=64)
+            gather(prod[:], pair[0], d, 0, V)
+            for h in range(HALVES):
+                turn(mid_first[:, h, :], prod[:, h * P : (h + 1) * P], (d, h) == (0, 0), (d, h) == (D - 2, HALVES - 1))
+        summed = [keep.tile([P, PACK, P], F32, name="summed%d" % h, align_bytes=64) for h in range(HALVES)]
         for h in range(HALVES):
-            nc.scalar.activation(
-                out=summed[h][:, :, 0 : LAST * 32], in_=acc_main[h][:].rearrange("v (p t) -> v t p", t=PACK), func=RELU
-            )
+            nc.scalar.copy(out=summed[h][:], in_=acc[h][:].rearrange("v (p t) -> v t p", t=PACK))
+        prod = keep.tile([P, V], F32, name="prod", tag="last_prods", align_bytes=64)
+        gather(prod[:], pair[1], 0, 0, V)
         for h in range(HALVES):
-            last_neighbours(len(units) - 1, h)
+            turn(mid_last[h][:], prod[:, h * P : (h + 1) * P], True, False)
+        for h in range(HALVES):
+            prod = prods.tile([P, P], F32, name="prod", align_bytes=64)
+            gather(prod[:], pair[1], 1, h * P, (h + 1) * P)
+            turn(mid_last[h][:], prod[:], False, True)
+        first_sums = keep.tile([P, HALVES, P], F32, name="first_sums", align_bytes=64)
+        nc.scalar.copy(out=first_sums[:], in_=mid_first[:])
+        last_sums = [keep.tile([P, P], F32, name="last_sums%d" % h, align_bytes=64) for h in range(HALVES)]
+        base = [banks.tile([P, 2, P], F32, name="base%d" % h, tag="acc%d" % h) for h in range(HALVES)]
+        for h in range(HALVES):
+            turn(base[h][:, 0, :], summed[h][:, 2, :], True, False)
+            turn(base[h][:, 1, :], summed[h][:, 3, :], False, False)
+            turn(base[h][:, 0, :], first_sums[:, h, :], False, False)
+        for h in range(HALVES):
+            nc.scalar.copy(out=last_sums[h][:], in_=mid_last[h][:])
+            turn(base[h][:, 1, :], last_sums[h][:], False, True)
+        last_prods = keep.tile([P, 2, V], F32, name="last_prods", align_bytes=64)
+        gather(last_prods[:, 0, :], pair[0], D - 1, 0, V)
+        for h in range(HALVES):
+            gather(last_prods[:, 1, h * P : (h + 1) * P], pair[1], D - 1, h * P, (h + 1) * P)
+
+        out_rows = out_0.rearrange("(p t) v -> p t v", t=PACK)
+        sums = keep.tile([P, PACK, V], F32, name="sums", align_bytes=64)
+        early = banks.tile([P, 2, V], F32, name="early")
+        for t in range(2):
+            for h in range(HALVES):
+                turn(early[:, t, h * P : (h + 1) * P], summed[h][:, t, :], (t, h) == (0, 0), (t, h) == (1, HALVES - 1))
+        nc.scalar.activation(out=sums[:, 0:2, :], in_=early[:], func=RELU)
+        nc.sync.dma_start(out=out_rows[:, 0:2, :], in_=sums[:, 0:2, :])
 
         out_words = keep.tile([P, V], I32, name="out_words", align_bytes=64)
         out_planes = keep.tile([P, V], U8, name="out_planes", align_bytes=64)
         result_bf = keep.tile([P, V, PACK], BF16, name="result_bf", align_bytes=64)
-        out_rows = out_0.rearrange("(p t) v -> p t v", t=PACK)
-        result = [keep.tile([P, PACK, P], F32, name="result%d" % h, align_bytes=64) for h in range(HALVES)]
-        dealt = [acc_last[h][:].rearrange("v (p t) -> v t p", t=PACK) for h in range(HALVES)]
-        nc.scalar.activation(out=summed[0][:, :, LAST * 32 : P], in_=dealt[0], func=RELU)
-        turned = banks.tile([P, PACK, P], F32, name="turned", tag="main0")
-        for t in range(PACK):
-            nc.tensor.transpose(turned[:, t, :], summed[0][:, t, :], ident[:])
-        nc.scalar.copy(out=result[0][:], in_=turned[:])
-        nc.sync.dma_start(out=out_rows[:, :, 0:P], in_=result[0][:])
-        nc.vector.tensor_scalar_max(summed[1][:, :, LAST * 32 : P], dealt[1], 0.0)
-        pairs = [ybanks.tile([P, 2, P], F32, name="ybank") for j in range(2)]
-        for t in range(PACK):
-            nc.tensor.transpose(pairs[t // 2][:, t % 2, :], summed[1][:, t, :], ident[:])
-        nc.vector.tensor_copy(out=result_bf[:, P:V, 0:2], in_=pairs[0][:].rearrange("p t c -> p c t"))
-        nc.scalar.copy(out=result[1][:, 2:4, :], in_=pairs[1][:])
-        nc.vector.tensor_copy(
-            out=result_bf[:, 0:P, :].rearrange("p (c i) t -> p c t i", i=4), in_=result[0][:].rearrange("p t (c i) -> p c t i", i=4)
-        )
-        nc.scalar.copy(out=result[1][:, 0:2, :], in_=pairs[0][:])
-        nc.vector.tensor_copy(out=result_bf[:, P:V, 2:4], in_=pairs[1][:].rearrange("p t c -> p c t"))
-        nc.sync.dma_start(out=out_rows[:, :, P:V], in_=result[1][:])
-        nc.vector.quantize_mx(out=out_words[:].bitcast(FP8X4), scales=out_planes[:], in_=result_bf[:].rearrange("p c t -> p (c t)"))
+        late = keep.tile([P, 2, V], F32, name="late", align_bytes=64)
+        halves = [slice(h * P, (h + 1) * P) for h in range(HALVES)]
+        for cols in halves:
+            nc.vector.tensor_tensor(sums[:, 2:4, cols], last_prods[:, :, cols], base[cols.start // P][:], ADD)
+        for cols in halves:
+            nc.vector.tensor_scalar_max(
+                result_bf[:, cols, :].rearrange("p (c i) t -> p c t i", i=4), sums[:, :, cols].rearrange("p t (c i) -> p c t i", i=4), 0.0
+            )
+        nc.scalar.activation(out=late[:], in_=sums[:, 2:4, :], func=RELU)
+        nc.sync.dma_start(out=out_rows[:, 2:4, :], in_=late[:])
+        for cols in halves:
+            nc.vector.quantize_mx(
+                out=out_words[:, cols].bitcast(FP8X4), scales=out_planes[:, cols], in_=result_bf[:, cols, :].rearrange("p c t -> p (c t)")
+            )
         nc.scalar.dma_start(out=out_1[0].rearrange("p c r -> p (c r)").bitcast(I32), in_=out_words[:])
         for quad in range(4):
             queue = nc.scalar if quad % 2 else nc.sync

@@ -23,6 +23,7 @@ HALVES = V // P
 FLOPS = 2 * K * N * S * D
 
 UNITS = D * CHUNKS
+DEEPER_FROM = 3
 DEALT_FROM = (D - 1) * CHUNKS
 
 
@@ -86,11 +87,9 @@ def tile_picked_zkp_three_po_kernel(tc, x_words, x_scales, w1, w2, w3, corr, off
                 load_w(u, 0, 1)
             elif u % 2 == 0:
                 load_w(u, 0, 2)
-            if u == DEALT_FROM - 1:
-                load_whole(0)
             load_w(u, 1, 1)
-            if u > CHUNKS and u % CHUNKS == 1:
-                load_corr(u // CHUNKS)
+        load_corr(1)
+        load_whole(0)
         load_whole(1)
         load_corr(D - 1)
 
@@ -157,7 +156,7 @@ def tile_picked_zkp_three_po_kernel(tc, x_words, x_scales, w1, w2, w3, corr, off
                 )
 
         def unload(u):
-            if u < DEALT_FROM - 1:
+            if u < 2:
                 tag = "raw%d_1" % (u + 1)
             else:
                 tag = "y%d" % u
@@ -175,8 +174,8 @@ def tile_picked_zkp_three_po_kernel(tc, x_words, x_scales, w1, w2, w3, corr, off
         def neighbour(u, d):
             if u in held:
                 prod = held[u][:, d, :]
-            elif (u, d) == (DEALT_FROM - 2, 1):
-                prod = keep.tile([P, V], F32, name="prod", tag="y%d" % (u + 1), align_bytes=64)[:]
+            elif (u, d) == (DEALT_FROM - 3, 1):
+                prod = keep.tile([P, V], F32, name="prod", tag="y%d" % (u + 2), align_bytes=64)[:]
             else:
                 prod = prods.tile([P, V], F32, name="prod", align_bytes=64)[:]
             gather(prod, u, d, 0, V)
@@ -221,12 +220,13 @@ def tile_picked_zkp_three_po_kernel(tc, x_words, x_scales, w1, w2, w3, corr, off
         nc.vector.tensor_copy(out=y[0][:, 0 : S // 2], in_=first[0][:])
         nc.scalar.copy(out=y[0][:, S // 2 : S], in_=first[1][:])
         for u in range(UNITS - 2):
-            if 0 < u < DEALT_FROM - 1:
+            if 0 < u <= DEEPER_FROM:
                 cast(u + 1, 0)
-                if u == DEALT_FROM - 2:
-                    cast_dealt(u + 2, 0)
                 finish(u + 1)
-            elif u == DEALT_FROM:
+            if DEEPER_FROM <= u < DEALT_FROM - 2:
+                cast(u + 2, 0)
+                finish(u + 2)
+            elif u == DEALT_FROM - 2 or u == DEALT_FROM:
                 cast_dealt(u + 2, 0)
             elif u == DEALT_FROM - 1 or u == DEALT_FROM + 1:
                 cast_dealt(u + 1, 1)

@@ -34,8 +34,8 @@ def tile_picked_zkp_three_po_kernel(tc, x_words, x_scales, w1, w2, w3, corr, off
         lists = ctx.enter_context(tc.tile_pool(name="lists", bufs=1))
         keep = ctx.enter_context(tc.tile_pool(name="keep", bufs=1))
         placed = ctx.enter_context(tc.tile_pool(name="placed", bufs=1))
-        ring = ctx.enter_context(tc.tile_pool(name="ring", bufs=4))
-        prods = ctx.enter_context(tc.tile_pool(name="prods", bufs=8))
+        ring = ctx.enter_context(tc.tile_pool(name="ring", bufs=UNITS))
+        prods = ctx.enter_context(tc.tile_pool(name="prods", bufs=D * UNITS))
         ybanks = ctx.enter_context(tc.psum_pool(name="ybanks", bufs=4))
         banks = ctx.enter_context(tc.psum_pool(name="banks", bufs=1))
 
@@ -180,12 +180,14 @@ def tile_picked_zkp_three_po_kernel(tc, x_words, x_scales, w1, w2, w3, corr, off
                 prod = prods.tile([P, V], F32, name="prod", align_bytes=64)[:]
             gather(prod, u, d, 0, V)
             for h in range(HALVES):
+                block = prod[:, h * P : (h + 1) * P]
                 if u < DEALT_FROM:
                     c = u % CHUNKS
-                    target = acc[h][:, c * P : (c + 1) * P]
+                    turn(acc[h][:, c * P : (c + 1) * P], block, (u, d) == (0, 0), False)
+                elif u == DEALT_FROM:
+                    turn(acc[h][:].rearrange("v (p t) -> v t p", t=PACK)[:, 0, :], block, False, d == D - 1)
                 else:
-                    target = acc[h][:].rearrange("v (p t) -> v t p", t=PACK)[:, u - DEALT_FROM, :]
-                turn(target, prod[:, h * P : (h + 1) * P], (u, d) == (0, 0), (u, d) == (UNITS - 3, D - 1))
+                    turn(mid_second[:, h, :], block, (d, h) == (0, 0), (d, h) == (D - 1, HALVES - 1))
 
         for g in range(PASSES):
             cast(0, g)
@@ -237,12 +239,32 @@ def tile_picked_zkp_three_po_kernel(tc, x_words, x_scales, w1, w2, w3, corr, off
                     held[u] = placed.tile([P, D, V], F32, name="held_prods", align_bytes=64, offset=64)
             if u > 0:
                 unload(u)
+            if u == DEALT_FROM + 1:
+                mid_second = ybanks.tile([P, HALVES, P], F32, name="ybank")
             for d in range(D):
                 neighbour(u, d)
 
         pair = (UNITS - 2, UNITS - 1)
         unload(pair[0])
         unload(pair[1])
+        summed = [keep.tile([P, PACK, P], F32, name="summed%d" % h, align_bytes=64) for h in range(HALVES)]
+        for h in range(HALVES):
+            nc.scalar.copy(out=summed[h][:], in_=acc[h][:].rearrange("v (p t) -> v t p", t=PACK))
+        early = banks.tile([P, 2, V], F32, name="early")
+        base = [banks.tile([P, 2, P], F32, name="base%d" % h, tag="acc%d" % h) for h in range(HALVES)]
+        for h in range(HALVES):
+            for t in range(2):
+                turn(early[:, t, h * P : (h + 1) * P], summed[h][:, t, :], (t, h) == (0, 0), False)
+                turn(base[h][:, t, :], summed[h][:, 2 + t, :], t == 0, False)
+        second_sums = keep.tile([P, HALVES, P], F32, name="second_sums", align_bytes=64)
+        nc.scalar.copy(out=second_sums[:], in_=mid_second[:])
+        for h in range(HALVES):
+            turn(early[:, 1, h * P : (h + 1) * P], second_sums[:, h, :], False, h == HALVES - 1)
+        out_rows = out_0.rearrange("(p t) v -> p t v", t=PACK)
+        sums = keep.tile([P, PACK, V], F32, name="sums", align_bytes=64)
+        nc.scalar.activation(out=sums[:, 0:2, :], in_=early[:], func=RELU)
+        nc.sync.dma_start(out=out_rows[:, 0:2, :], in_=sums[:, 0:2, :])
+
         mid_first = banks.tile([P, HALVES, P], F32, name="mid_first")
         mid_last = [ybanks.tile([P, P], F32, name="ybank") for h in range(HALVES)]
         for d in range(D - 1):
@@ -250,9 +272,6 @@ def tile_picked_zkp_three_po_kernel(tc, x_words, x_scales, w1, w2, w3, corr, off
             gather(prod[:], pair[0], d, 0, V)
             for h in range(HALVES):
                 turn(mid_first[:, h, :], prod[:, h * P : (h + 1) * P], (d, h) == (0, 0), (d, h) == (D - 2, HALVES - 1))
-        summed = [keep.tile([P, PACK, P], F32, name="summed%d" % h, align_bytes=64) for h in range(HALVES)]
-        for h in range(HALVES):
-            nc.scalar.copy(out=summed[h][:], in_=acc[h][:].rearrange("v (p t) -> v t p", t=PACK))
         prod = keep.tile([P, V], F32, name="prod", tag="last_prods", align_bytes=64)
         gather(prod[:], pair[1], 0, 0, V)
         for h in range(HALVES):
@@ -264,10 +283,7 @@ def tile_picked_zkp_three_po_kernel(tc, x_words, x_scales, w1, w2, w3, corr, off
         first_sums = keep.tile([P, HALVES, P], F32, name="first_sums", align_bytes=64)
         nc.scalar.copy(out=first_sums[:], in_=mid_first[:])
         last_sums = [keep.tile([P, P], F32, name="last_sums%d" % h, align_bytes=64) for h in range(HALVES)]
-        base = [banks.tile([P, 2, P], F32, name="base%d" % h, tag="acc%d" % h) for h in range(HALVES)]
         for h in range(HALVES):
-            turn(base[h][:, 0, :], summed[h][:, 2, :], True, False)
-            turn(base[h][:, 1, :], summed[h][:, 3, :], False, False)
             turn(base[h][:, 0, :], first_sums[:, h, :], False, False)
         for h in range(HALVES):
             nc.scalar.copy(out=last_sums[h][:], in_=mid_last[h][:])
@@ -276,15 +292,6 @@ def tile_picked_zkp_three_po_kernel(tc, x_words, x_scales, w1, w2, w3, corr, off
         gather(last_prods[:, 0, :], pair[0], D - 1, 0, V)
         for h in range(HALVES):
             gather(last_prods[:, 1, h * P : (h + 1) * P], pair[1], D - 1, h * P, (h + 1) * P)
-
-        out_rows = out_0.rearrange("(p t) v -> p t v", t=PACK)
-        sums = keep.tile([P, PACK, V], F32, name="sums", align_bytes=64)
-        early = banks.tile([P, 2, V], F32, name="early")
-        for t in range(2):
-            for h in range(HALVES):
-                turn(early[:, t, h * P : (h + 1) * P], summed[h][:, t, :], (t, h) == (0, 0), (t, h) == (1, HALVES - 1))
-        nc.scalar.activation(out=sums[:, 0:2, :], in_=early[:], func=RELU)
-        nc.sync.dma_start(out=out_rows[:, 0:2, :], in_=sums[:, 0:2, :])
 
         out_words = keep.tile([P, V], I32, name="out_words", align_bytes=64)
         out_planes = keep.tile([P, V], U8, name="out_planes", align_bytes=64)
@@ -297,8 +304,9 @@ def tile_picked_zkp_three_po_kernel(tc, x_words, x_scales, w1, w2, w3, corr, off
             nc.vector.tensor_scalar_max(
                 result_bf[:, cols, :].rearrange("p (c i) t -> p c t i", i=4), sums[:, :, cols].rearrange("p t (c i) -> p c t i", i=4), 0.0
             )
-        nc.scalar.activation(out=late[:], in_=sums[:, 2:4, :], func=RELU)
-        nc.sync.dma_start(out=out_rows[:, 2:4, :], in_=late[:])
+        for cols in halves:
+            nc.scalar.activation(out=late[:, :, cols], in_=sums[:, 2:4, cols], func=RELU)
+            nc.sync.dma_start(out=out_rows[:, 2:4, cols], in_=late[:, :, cols])
         for cols in halves:
             nc.vector.quantize_mx(
                 out=out_words[:, cols].bitcast(FP8X4), scales=out_planes[:, cols], in_=result_bf[:, cols, :].rearrange("p c t -> p (c t)")

@@ -24,6 +24,7 @@ FLOPS = 2 * K * N * S * D
 
 UNITS = D * CHUNKS
 DEEPER_FROM = 3
+HALVED = (2, 8, 10)
 DEALT_FROM = (D - 1) * CHUNKS
 
 
@@ -43,7 +44,7 @@ def tile_picked_zkp_three_po_kernel(tc, x_words, x_scales, w1, w2, w3, corr, off
         pos_t = [lists.tile([P, V // 16], U16, name="pos_t%d" % d) for d in range(D)]
         x_all = [keep.tile([P, T], I32, name="x_all%d" % g, align_bytes=64) for g in range(PASSES)]
         xs_all = keep.tile([P, T], U8, name="xs_all", align_bytes=64)
-        corr_t = [keep.tile([P, D, V], F32, name="corr_t%d" % q, align_bytes=64) for q in range(D)]
+        near = {}
         raw = {}
 
         def load_x(g):
@@ -63,8 +64,11 @@ def tile_picked_zkp_three_po_kernel(tc, x_words, x_scales, w1, w2, w3, corr, off
             whole.append(keep.tile([P, PACK, N], F32, name="whole%d" % g, align_bytes=64))
             nc.sync.dma_start(out=whole[g][:], in_=weights[D - 1][g * 512 : (g + 1) * 512, :].rearrange("(p t) n -> p t n", t=PACK))
 
-        def load_corr(q):
-            nc.sync.dma_start(out=corr_t[q][:], in_=corr[D * q : D * q + D].rearrange("d p v -> p d v"))
+        def load_corr(lo, hi):
+            tile = keep.tile([P, hi - lo, V], F32, name="corr%d" % lo, align_bytes=64)
+            nc.sync.dma_start(out=tile[:], in_=corr[lo:hi].rearrange("d p v -> p d v"))
+            for i in range(lo, hi):
+                near[i] = tile[:, i - lo, :]
 
         nc.gpsimd.memset(xs_all[:].bitcast(I32), 0)
         nc.sync.dma_start(offs_t[:], offs)
@@ -81,17 +85,19 @@ def tile_picked_zkp_three_po_kernel(tc, x_words, x_scales, w1, w2, w3, corr, off
         load_w(1, 1, 1)
         for d, pos in enumerate((pos1, pos2, pos3)):
             nc.sync.dma_start(pos_t[d][:], pos)
-        load_corr(0)
+        load_corr(0, D - 1)
         for u in range(2, DEALT_FROM):
             if u < CHUNKS:
                 load_w(u, 0, 1)
             elif u % 2 == 0:
                 load_w(u, 0, 2)
             load_w(u, 1, 1)
-        load_corr(1)
+            if u == 2:
+                load_corr(D - 1, D)
+        load_corr(D, 2 * D)
         load_whole(0)
         load_whole(1)
-        load_corr(D - 1)
+        load_corr(2 * D, D * D)
 
         ident_raw = keep.tile([P, P], F32, name="ident_raw")
         make_identity(nc, ident_raw[:])
@@ -142,32 +148,38 @@ def tile_picked_zkp_three_po_kernel(tc, x_words, x_scales, w1, w2, w3, corr, off
 
         def multiply(u):
             w_codes, w_planes = codes[u]
-            ybank[u] = ybanks.tile([P, S], F32, name="ybank")
-            for g in range(PASSES):
-                cols = slice(g * P, (g + 1) * P)
-                nc.tensor.matmul_mx(
-                    out=ybank[u][:],
-                    lhsT=w_codes[:, cols].bitcast(FP8X4),
-                    lhsT_scale=w_planes[:, cols],
-                    rhs=x_codes[g][:].bitcast(FP8X4),
-                    rhs_scale=x_planes[4 * g : P, :],
-                    start=(g == 0),
-                    stop=(g == PASSES - 1),
-                )
+            width = S // 2 if u in HALVED else S
+            ybank[u] = []
+            for lo in range(0, S, width):
+                part = slice(lo, lo + width)
+                bank = ybanks.tile([P, width], F32, name="ybank")
+                ybank[u].append((part, bank))
+                for g in range(PASSES):
+                    cols = slice(g * P, (g + 1) * P)
+                    nc.tensor.matmul_mx(
+                        out=bank[:],
+                        lhsT=w_codes[:, cols].bitcast(FP8X4),
+                        lhsT_scale=w_planes[:, cols],
+                        rhs=x_codes[g][:, part].bitcast(FP8X4),
+                        rhs_scale=x_planes[4 * g : P, part],
+                        start=(g == 0),
+                        stop=(g == PASSES - 1),
+                    )
 
         def unload(u):
-            if u < 2:
+            if u < 3:
                 tag = "raw%d_1" % (u + 1)
             else:
                 tag = "y%d" % u
             y[u] = keep.tile([P, S], F32, name="y", tag=tag, align_bytes=64)
-            nc.scalar.copy(out=y[u][:], in_=ybank[u][:])
+            for part, bank in ybank[u]:
+                nc.scalar.copy(out=y[u][:, part], in_=bank[:])
 
         def turn(target, block, first, final):
             nc.tensor.matmul(out=target, lhsT=block, rhs=ident[:], is_transpose=True, start=first, stop=final)
 
         def gather(prod, u, d, lo, hi):
-            nc.vector.tensor_tensor(prod, y[u][:].indirect(pos_t[d][:, lo // 16 : hi // 16]), corr_t[u // CHUNKS][:, d, lo:hi], MULT)
+            nc.vector.tensor_tensor(prod, y[u][:].indirect(pos_t[d][:, lo // 16 : hi // 16]), near[D * (u // CHUNKS) + d][:, lo:hi], MULT)
 
         held = {}
 
@@ -311,7 +323,7 @@ def tile_picked_zkp_three_po_kernel(tc, x_words, x_scales, w1, w2, w3, corr, off
             nc.vector.quantize_mx(
                 out=out_words[:, cols].bitcast(FP8X4), scales=out_planes[:, cols], in_=result_bf[:, cols, :].rearrange("p c t -> p (c t)")
             )
-        nc.scalar.dma_start(out=out_1[0].rearrange("p c r -> p (c r)").bitcast(I32), in_=out_words[:])
+            nc.scalar.dma_start(out=out_1[0].rearrange("p c r -> p (c r)").bitcast(I32)[:, cols], in_=out_words[:, cols])
         for quad in range(4):
             queue = nc.scalar if quad % 2 else nc.sync
             queue.dma_start(

@@ -78,10 +78,9 @@ def tile_picked_zkp_three_po_kernel(tc, x_words, x_scales, w1, w2, w3, corr, off
                 out=xs_all[32 * quad : 32 * quad + 4 * PASSES, :].bitcast(I32),
                 in_=x_scales[:, 4 * quad : 4 * quad + 4, :].bitcast(I32),
             )
-        load_w(0, 0, 1)
+        load_w(0, 0, 2)
         load_w(0, 1, 1)
         load_x(1)
-        load_w(1, 0, 1)
         load_w(1, 1, 1)
         for d, pos in enumerate((pos1, pos2, pos3)):
             nc.sync.dma_start(pos_t[d][:], pos)
@@ -99,10 +98,8 @@ def tile_picked_zkp_three_po_kernel(tc, x_words, x_scales, w1, w2, w3, corr, off
         load_whole(1)
         load_corr(2 * D, D * D)
 
-        ident_raw = keep.tile([P, P], F32, name="ident_raw")
-        make_identity(nc, ident_raw[:])
         ident = keep.tile([P, P], F32, name="ident")
-        nc.scalar.activation(out=ident[:], in_=ident_raw[:], func=RELU)
+        make_identity(nc, ident[:])
 
         x_codes = [keep.tile([P, S], I32, name="x_codes0", align_bytes=64)]
         x_planes = keep.tile([P, S], U8, name="x_planes", align_bytes=64)

@@ -11,6 +11,7 @@ U16 = mybir.dt.uint16
 U8 = mybir.dt.uint8
 FP8X4 = mybir.dt.float8_e4m3fn_x4
 RELU = mybir.ActivationFunctionType.Relu
+COPY = mybir.ActivationFunctionType.Copy
 MULT = mybir.AluOpType.mult
 ADD = mybir.AluOpType.add
 
@@ -23,9 +24,25 @@ HALVES = V // P
 FLOPS = 2 * K * N * S * D
 
 UNITS = D * CHUNKS
-DEEPER_FROM = 3
-HALVED = (2, 8, 10)
 DEALT_FROM = (D - 1) * CHUNKS
+PAIRS = UNITS // 2
+EXTRA = ((1,), (3,), (4,), (6,), ())
+SCALAR_CASTS = ()
+HELD = {
+    ("G", 1, 0): "raw2_1",
+    ("G", 1, 1): "raw2_1",
+    ("A", 0, 1): "raw2_1",
+    ("A", 1, 2): "rounded2_1",
+    ("G", 3, 0): "rounded4_1",
+    ("G", 3, 1): "rounded4_1",
+    ("G", 5, 0): "rounded6_1",
+    ("G", 4, 1): "rounded6_1",
+    ("A", 6, 2): "last_raw",
+    ("A", 7, 2): "last_raw",
+    ("A", 7, 1): "last_raw",
+    ("G", 7, 0): "rounded8_1",
+    ("G", 6, 1): "rounded8_1",
+}
 
 
 def tile_picked_zkp_three_po_kernel(tc, x_words, x_scales, w1, w2, w3, corr, offs, pos1, pos2, pos3, out_0, out_1, out_2):
@@ -35,9 +52,9 @@ def tile_picked_zkp_three_po_kernel(tc, x_words, x_scales, w1, w2, w3, corr, off
         lists = ctx.enter_context(tc.tile_pool(name="lists", bufs=1))
         keep = ctx.enter_context(tc.tile_pool(name="keep", bufs=1))
         placed = ctx.enter_context(tc.tile_pool(name="placed", bufs=1))
-        ring = ctx.enter_context(tc.tile_pool(name="ring", bufs=UNITS))
-        prods = ctx.enter_context(tc.tile_pool(name="prods", bufs=D * UNITS))
-        ybanks = ctx.enter_context(tc.psum_pool(name="ybanks", bufs=4))
+        prods = ctx.enter_context(tc.tile_pool(name="prods", bufs=D * UNITS + 2))
+        ybanks = ctx.enter_context(tc.psum_pool(name="ybanks", bufs=2))
+        sbanks = ctx.enter_context(tc.psum_pool(name="sbanks", bufs=2))
         banks = ctx.enter_context(tc.psum_pool(name="banks", bufs=1))
 
         offs_t = lists.tile([P, S // 16], U16, name="offs_t")
@@ -46,29 +63,30 @@ def tile_picked_zkp_three_po_kernel(tc, x_words, x_scales, w1, w2, w3, corr, off
         xs_all = keep.tile([P, T], U8, name="xs_all", align_bytes=64)
         near = {}
         raw = {}
+        loaded = {}
 
         def load_x(g):
             nc.sync.dma_start(out=x_all[g][:], in_=x_words[g].rearrange("p n t -> p (n t)").bitcast(I32))
 
         def load_w(u, g, count):
             q, c = divmod(u, CHUNKS)
-            tile = keep.tile([P, PACK, count * P], F32, name="raw", tag="raw%d_%d" % (u, g), align_bytes=64)
+            if (u, g) == (DEALT_FROM, 1):
+                tile = placed.tile([P, PACK, count * P], F32, name="last_raw", align_bytes=64, offset=0)
+            else:
+                tile = keep.tile([P, PACK, count * P], F32, name="raw", tag="raw%d_%d" % (u, g), align_bytes=64)
             part = weights[q][g * 512 : (g + 1) * 512, c * P : (c + count) * P]
             nc.sync.dma_start(out=tile[:], in_=part.rearrange("(p t) n -> p t n", t=PACK))
             for j in range(count):
                 raw[(u + j, g)] = tile[:, :, j * P : (j + 1) * P]
+            loaded[(u, g)] = tile
+            return tile
 
-        whole = []
-
-        def load_whole(g):
-            whole.append(keep.tile([P, PACK, N], F32, name="whole%d" % g, align_bytes=64))
-            nc.sync.dma_start(out=whole[g][:], in_=weights[D - 1][g * 512 : (g + 1) * 512, :].rearrange("(p t) n -> p t n", t=PACK))
-
-        def load_corr(lo, hi):
-            tile = keep.tile([P, hi - lo, V], F32, name="corr%d" % lo, align_bytes=64)
-            nc.sync.dma_start(out=tile[:], in_=corr[lo:hi].rearrange("d p v -> p d v"))
-            for i in range(lo, hi):
-                near[i] = tile[:, i - lo, :]
+        def load_corr(*entries):
+            tile = keep.tile([P, len(entries), V], F32, name="corr%d" % entries[0], align_bytes=64)
+            step = entries[1] - entries[0] if len(entries) > 1 else 1
+            nc.sync.dma_start(out=tile[:], in_=corr[entries[0] : entries[-1] + 1 : step].rearrange("d p v -> p d v"))
+            for j, i in enumerate(entries):
+                near[i] = tile[:, j, :]
 
         nc.gpsimd.memset(xs_all[:].bitcast(I32), 0)
         nc.sync.dma_start(offs_t[:], offs)
@@ -78,35 +96,36 @@ def tile_picked_zkp_three_po_kernel(tc, x_words, x_scales, w1, w2, w3, corr, off
                 out=xs_all[32 * quad : 32 * quad + 4 * PASSES, :].bitcast(I32),
                 in_=x_scales[:, 4 * quad : 4 * quad + 4, :].bitcast(I32),
             )
-        load_w(0, 0, 2)
+        load_w(0, 0, 1)
         load_w(0, 1, 1)
         load_x(1)
+        load_w(1, 0, 1)
         load_w(1, 1, 1)
         for d, pos in enumerate((pos1, pos2, pos3)):
             nc.sync.dma_start(pos_t[d][:], pos)
-        load_corr(0, D - 1)
-        for u in range(2, DEALT_FROM):
-            if u < CHUNKS:
-                load_w(u, 0, 1)
-            elif u % 2 == 0:
-                load_w(u, 0, 2)
-            load_w(u, 1, 1)
-            if u == 2:
-                load_corr(D - 1, D)
-        load_corr(D, 2 * D)
-        load_whole(0)
-        load_whole(1)
-        load_corr(2 * D, D * D)
+        corr_rows = keep.tile([P, P], F32, name="corr_rows", align_bytes=64)
+        nc.sync.dma_start(out=corr_rows[:], in_=corr[0:8, 0:8, :].rearrange("i r (h v) -> i (r h) v", h=HALVES))
+        load_w(2, 0, 2)
+        load_corr(1, 2)
+        load_w(2, 1, 2)
+        load_w(4, 0, 2)
+        load_w(4, 1, 2)
+        load_w(6, 0, 2)
+        load_w(6, 1, 2)
+        load_corr(4, 5)
+        whole = [load_w(DEALT_FROM, g, CHUNKS) for g in range(PASSES)]
+        load_corr(6, 7, 8)
 
         ident = keep.tile([P, P], F32, name="ident")
         make_identity(nc, ident[:])
+
+        def turn(target, block, first, final):
+            nc.tensor.matmul(out=target, lhsT=block, rhs=ident[:], is_transpose=True, start=first, stop=final)
 
         x_codes = [keep.tile([P, S], I32, name="x_codes0", align_bytes=64)]
         x_planes = keep.tile([P, S], U8, name="x_planes", align_bytes=64)
         nc.vector.tensor_copy(x_codes[0][:].bitcast(U32), x_all[0][:].bitcast(U32).indirect(offs_t[:]))
         nc.vector.tensor_copy(x_planes[:], xs_all[:].indirect(offs_t[:]))
-
-        acc = [banks.tile([P, N], F32, name="acc%d" % h, tag="acc%d" % h) for h in range(HALVES)]
 
         rounded = {}
         codes = {}
@@ -114,96 +133,66 @@ def tile_picked_zkp_three_po_kernel(tc, x_words, x_scales, w1, w2, w3, corr, off
         y = {}
 
         def cast(u, g):
-            if g == 0:
-                rounded[u] = keep.tile([P, PASSES, P, PACK], BF16, name="rounded", tag="rounded%d" % u, align_bytes=64)[:]
+            rounded[(u, g)] = keep.tile([P, P, PACK], BF16, name="rounded", tag="rounded%d_%d" % (u, g), align_bytes=64)
             nc.scalar.copy(
-                out=rounded[u][:, g].rearrange("p (c i) t -> p c t i", i=4),
-                in_=raw[(u, g)].rearrange("p t (c i) -> p c t i", i=4),
+                out=rounded[(u, g)][:].rearrange("p (c i) t -> p c t i", i=4), in_=raw[(u, g)].rearrange("p t (c i) -> p c t i", i=4)
             )
 
-        def cast_dealt(u, g):
-            if g == 0:
-                start = 3072 if u == DEALT_FROM else 7104
-                both = placed.tile([P, 2, PASSES, P, PACK], BF16, name="rounded", tag="rounded%d" % u, align_bytes=64, offset=start)
-                rounded[(u, u + 1)] = both
-                rounded[u], rounded[u + 1] = both[:, 0], both[:, 1]
+        def cast_pair(u, g):
+            both = keep.tile([P, 2 * P, PACK], BF16, name="rounded", tag="rounded%d_%d" % (u, g), align_bytes=64)
+            rounded[(u, g)] = both
             s = u - DEALT_FROM
-            nc.scalar.copy(
-                out=rounded[(u, u + 1)][:, :, g].rearrange("p s m t -> p m t s"),
-                in_=whole[g][:].rearrange("p t (m s) -> p m t s", s=PACK)[:, :, :, s : s + 2],
-            )
+            copy = nc.scalar.copy if (u, g) in SCALAR_CASTS else nc.vector.tensor_copy
+            if s < 0:
+                copy(
+                    out=both[:].rearrange("p (c i) t -> p c t i", i=4), in_=loaded[(u, g)][:].rearrange("p t (c i) -> p c t i", i=4)
+                )
+            else:
+                copy(
+                    out=both[:].rearrange("p (s m) t -> p m t s", s=2),
+                    in_=whole[g][:].rearrange("p t (m s) -> p m t s", s=PACK)[:, :, :, s : s + 2],
+                )
 
-        def quantise(u, g0, g1):
-            if g0 == 0:
-                w_codes = ring.tile([P, PASSES * P], I32, name="w_codes", align_bytes=64)
-                w_planes = ring.tile([P, PASSES * P], U8, name="w_planes", align_bytes=64)
-                codes[u] = (w_codes, w_planes)
-            w_codes, w_planes = codes[u]
-            a, b = g0 * P, g1 * P
-            source = rounded[u].rearrange("p g c t -> p (g c t)")[:, PACK * a : PACK * b]
-            nc.vector.quantize_mx(out=w_codes[:, a:b].bitcast(FP8X4), scales=w_planes[:, a:b], in_=source)
+        def quantise(u, g):
+            width = rounded[(u, g)].shape[1]
+            if (u, g) == (UNITS - 2, 0):
+                w_codes = placed.tile([P, width], I32, name="held_codes", align_bytes=64, offset=7 * V * 4)
+            else:
+                w_codes = keep.tile([P, width], I32, name="w_codes", tag="w_codes%d_%d" % (u, g), align_bytes=64)
+            w_planes = keep.tile([P, width], U8, name="w_planes", tag="w_planes%d_%d" % (u, g), align_bytes=64)
+            nc.vector.quantize_mx(out=w_codes[:].bitcast(FP8X4), scales=w_planes[:], in_=rounded[(u, g)][:].rearrange("p c t -> p (c t)"))
+            for j in range(width // P):
+                codes[(u + j, g)] = (w_codes[:, j * P : (j + 1) * P], w_planes[:, j * P : (j + 1) * P])
+
+        def one_pass(bank, u, g, part):
+            w_codes, w_planes = codes[(u, g)]
+            nc.tensor.matmul_mx(
+                out=bank,
+                lhsT=w_codes.bitcast(FP8X4),
+                lhsT_scale=w_planes,
+                rhs=x_codes[g][:, part].bitcast(FP8X4),
+                rhs_scale=x_planes[4 * g : P, part],
+                start=(g == 0),
+                stop=(g == PASSES - 1),
+            )
 
         def multiply(u):
-            w_codes, w_planes = codes[u]
-            width = S // 2 if u in HALVED else S
-            ybank[u] = []
-            for lo in range(0, S, width):
-                part = slice(lo, lo + width)
-                bank = ybanks.tile([P, width], F32, name="ybank")
-                ybank[u].append((part, bank))
-                for g in range(PASSES):
-                    cols = slice(g * P, (g + 1) * P)
-                    nc.tensor.matmul_mx(
-                        out=bank[:],
-                        lhsT=w_codes[:, cols].bitcast(FP8X4),
-                        lhsT_scale=w_planes[:, cols],
-                        rhs=x_codes[g][:, part].bitcast(FP8X4),
-                        rhs_scale=x_planes[4 * g : P, part],
-                        start=(g == 0),
-                        stop=(g == PASSES - 1),
-                    )
+            ybank[u] = ybanks.tile([P, S], F32, name="ybank")
+            for g in range(PASSES):
+                one_pass(ybank[u][:], u, g, slice(0, S))
 
         def unload(u):
-            if u < 3:
-                tag = "raw%d_1" % (u + 1)
-            else:
-                tag = "y%d" % u
-            y[u] = keep.tile([P, S], F32, name="y", tag=tag, align_bytes=64)
-            for part, bank in ybank[u]:
-                nc.scalar.copy(out=y[u][:, part], in_=bank[:])
-
-        def turn(target, block, first, final):
-            nc.tensor.matmul(out=target, lhsT=block, rhs=ident[:], is_transpose=True, start=first, stop=final)
+            y[u] = keep.tile([P, S], F32, name="y", tag="y%d" % u, align_bytes=64)
+            nc.scalar.copy(out=y[u][:], in_=ybank[u][:])
 
         def gather(prod, u, d, lo, hi):
             nc.vector.tensor_tensor(prod, y[u][:].indirect(pos_t[d][:, lo // 16 : hi // 16]), near[D * (u // CHUNKS) + d][:, lo:hi], MULT)
 
-        held = {}
-
-        def neighbour(u, d):
-            if u in held:
-                prod = held[u][:, d, :]
-            elif (u, d) == (DEALT_FROM - 3, 1):
-                prod = keep.tile([P, V], F32, name="prod", tag="y%d" % (u + 2), align_bytes=64)[:]
-            else:
-                prod = prods.tile([P, V], F32, name="prod", align_bytes=64)[:]
-            gather(prod, u, d, 0, V)
-            for h in range(HALVES):
-                block = prod[:, h * P : (h + 1) * P]
-                if u < DEALT_FROM:
-                    c = u % CHUNKS
-                    turn(acc[h][:, c * P : (c + 1) * P], block, (u, d) == (0, 0), False)
-                elif u == DEALT_FROM:
-                    turn(acc[h][:].rearrange("v (p t) -> v t p", t=PACK)[:, 0, :], block, False, d == D - 1)
-                else:
-                    turn(mid_second[:, h, :], block, (d, h) == (0, 0), (d, h) == (D - 1, HALVES - 1))
-
         for g in range(PASSES):
             cast(0, g)
-            quantise(0, g, g + 1)
+            quantise(0, g)
         x_codes.append(keep.tile([P, S], I32, name="x_codes1", tag="raw0_1", align_bytes=64))
-        w_codes, w_planes = codes[0]
-        first = [ybanks.tile([P, S // 2], F32, name="ybank") for j in range(2)]
+        first = [sbanks.tile([P, S // 2], F32, name="sbank") for j in range(2)]
         for g in range(PASSES):
             for j in range(2):
                 part = slice(j * S // 2, (j + 1) * S // 2)
@@ -211,70 +200,148 @@ def tile_picked_zkp_three_po_kernel(tc, x_words, x_scales, w1, w2, w3, corr, off
                     nc.vector.tensor_copy(
                         x_codes[g][:, part].bitcast(U32), x_all[g][:].bitcast(U32).indirect(offs_t[:, 16 * j : 16 * j + 16])
                     )
-                nc.tensor.matmul_mx(
-                    out=first[j][:],
-                    lhsT=w_codes[:, g * P : (g + 1) * P].bitcast(FP8X4),
-                    lhsT_scale=w_planes[:, g * P : (g + 1) * P],
-                    rhs=x_codes[g][:, part].bitcast(FP8X4),
-                    rhs_scale=x_planes[4 * g : P, part],
-                    start=(g == 0),
-                    stop=(g == PASSES - 1),
-                )
-        def finish(u):
-            cast(u, 1)
-            quantise(u, 0, PASSES)
-            multiply(u)
-
+                one_pass(first[j][:], 0, g, part)
         cast(1, 0)
-        finish(1)
-        y[0] = keep.tile([P, S], F32, name="y", tag="raw1_1", align_bytes=64)
-        nc.vector.tensor_copy(out=y[0][:, 0 : S // 2], in_=first[0][:])
-        nc.scalar.copy(out=y[0][:, S // 2 : S], in_=first[1][:])
-        for u in range(UNITS - 2):
-            if 0 < u <= DEEPER_FROM:
-                cast(u + 1, 0)
-                finish(u + 1)
-            if DEEPER_FROM <= u < DEALT_FROM - 2:
-                cast(u + 2, 0)
-                finish(u + 2)
-            elif u == DEALT_FROM - 2 or u == DEALT_FROM:
-                cast_dealt(u + 2, 0)
-            elif u == DEALT_FROM - 1 or u == DEALT_FROM + 1:
-                cast_dealt(u + 1, 1)
-                for j in range(1, 3):
-                    quantise(u + j, 0, PASSES)
-                    multiply(u + j)
+        cast(1, 1)
+        y[0] = keep.tile([P, S], F32, name="y", tag="y0", align_bytes=64)
+        for j in range(2):
+            nc.scalar.copy(out=y[0][:, j * S // 2 : (j + 1) * S // 2], in_=first[j][:])
+        quantise(1, 0)
+        quantise(1, 1)
+        multiply(1)
+
+        rows_turned = banks.tile([P, P], F32, name="rows_turned", tag="planes0")
+        turn(rows_turned[:], corr_rows[:], True, True)
+        near_cols = keep.tile([P, 8, HALVES], F32, name="near_cols", align_bytes=64)
+        nc.scalar.copy(out=near_cols[:], in_=rows_turned[:].rearrange("v (i r h) -> v i r h", i=8, h=HALVES)[:, :, 0, :])
+
+        acc = [banks.tile([P, N], F32, name="acc%d" % h, tag="acc%d" % h) for h in range(HALVES)]
+        planes = [banks.tile([P, 2, V], F32, name="planes%d" % a, tag="planes%d" % a) for a in range(2)]
+        acc_open = [False]
+        planes_open = [False, False]
+        sbank = {}
+        scaled = {}
+
+        def turn_back(tile, t, h, final):
+            turn(planes[t // 2][:, t % 2, h * P : (h + 1) * P], tile, not planes_open[t // 2], final)
+            planes_open[t // 2] = True
+
+        def fetch(plain, u, d, bank, first, final):
+            nc.scalar.activation(plain[:], y[u][:].indirect(pos_t[d][:]), COPY)
+            for h in range(HALVES):
+                turn(bank[:, h, :], plain[:, h * P : (h + 1) * P], first and h == 0, final and h == HALVES - 1)
+
+        def fetch_pair(pair):
+            both = sbanks.tile([P, HALVES, 2, P], F32, name="sbank")
+            extra = EXTRA[pair]
+            more = sbanks.tile([P, HALVES, len(extra), P], F32, name="sbank") if extra else None
+            terms = [(2 * pair, 0), (2 * pair + 1, 0)] + [(u, 1) for u in extra]
+            if len(extra) == 2:
+                terms = sorted(terms)
+            for u, d in terms:
+                if d == 0:
+                    fetch(spot("G", u, d), u, d, both[:, :, u % 2, :], u % 2 == 0, u % 2 == 1)
+                else:
+                    fetch(spot("G", u, d), u, d, more[:, :, u - extra[0], :], u == extra[0], u == extra[-1])
+            sbank[pair] = (both, more)
+
+        def scale(key, bank, u, count, d):
+            if key not in scaled:
+                scaled[key] = keep.tile([P, HALVES, PACK, P], F32, name="scaled%s" % key, align_bytes=64)
+            q, c = divmod(u, CHUNKS)
+            for h in range(HALVES):
+                factor = near_cols[:, D * q + d, h : h + 1]
                 if u < DEALT_FROM:
-                    held[u] = placed.tile([P, D, V], F32, name="held_prods", align_bytes=64, offset=64)
-            if u > 0:
+                    rows = slice(c * P // PACK, (c + count) * P // PACK)
+                    nc.scalar.activation(scaled[key][:, h, :, rows], bank[:, h].rearrange("v (p t) -> v t p", t=PACK), COPY, scale=factor)
+                else:
+                    nc.scalar.activation(scaled[key][:, h, c : c + count, :].rearrange("v t p -> v (t p)"), bank[:, h], COPY, scale=factor)
+
+        def scale_pair(pair):
+            both, more = sbank[pair]
+            scale("a%d" % (pair // 2), both[:].rearrange("v h j m -> v h (j m)"), 2 * pair, 2, 0)
+            if more is not None:
+                scale("b%d" % (pair // 4), more[:].rearrange("v h j m -> v h (j m)"), EXTRA[pair][0], len(EXTRA[pair]), 1)
+
+        def add_pair(pair):
+            keys = ["a%d" % (pair // 2), "b%d" % (pair // 4)]
+            counts = [(0, 0), (PACK, 0), (0, 0), (PACK, PACK), (2, len(EXTRA[4]))][pair]
+            for key, count in zip(keys, counts):
+                for h in range(HALVES):
+                    for t in range(count):
+                        turn_back(scaled[key][:, h, t, :], t, h, False)
+
+        def neighbour(prod, u, d, final):
+            gather(prod, u, d, 0, V)
+            for h in range(HALVES):
+                block = prod[:, h * P : (h + 1) * P]
+                if u < DEALT_FROM:
+                    c = u % CHUNKS
+                    turn(acc[h][:, c * P : (c + 1) * P], block, not acc_open[0], False)
+                else:
+                    turn(acc[h][:].rearrange("v (p t) -> v t p", t=PACK)[:, u - DEALT_FROM, :], block, False, final)
+            acc_open[0] = True
+
+        later = {}
+
+        def spot(*key):
+            if key not in HELD:
+                return prods.tile([P, V], F32, name="prod", align_bytes=64)[:]
+            tag = HELD[key]
+            mates = [other for other in HELD if HELD[other] == tag]
+            if tag == "last_raw":
+                return placed.tile([P, V], F32, name="later%d" % mates.index(key), align_bytes=64, offset=mates.index(key) * V * 4)[:]
+            if tag not in later:
+                later[tag] = keep.tile([P, len(mates), V], F32, name="later", tag=tag, align_bytes=64)
+            return later[tag][:, mates.index(key), :]
+
+        for p in range(PAIRS - 1):
+            u = 2 * p
+            mine = [(u, 2), (u, 1), (u + 1, 2), (u + 1, 1)]
+            mine = [term for term in mine if term[1] == 2 or term[0] not in EXTRA[p]]
+            if p < 4:
+                cast_pair(u + 2, 0)
+                if p == 3:
+                    cast_pair(u + 4, 0)
+                cast_pair(u + 2, 1)
+                quantise(u + 2, 0)
+                if p == 3:
+                    cast_pair(u + 4, 1)
+            if p > 0:
                 unload(u)
-            if u == DEALT_FROM + 1:
-                mid_second = ybanks.tile([P, HALVES, P], F32, name="ybank")
-            for d in range(D):
-                neighbour(u, d)
+            unload(u + 1)
+            if p > 0:
+                scale_pair(p - 1)
+            if p < 4:
+                quantise(u + 2, 1)
+                for j in range(2):
+                    multiply(u + 2 + j)
+            if p == 4:
+                for j in range(2):
+                    multiply(u + 2 + j)
+                    unload(u + 2 + j)
+            fetch_pair(p)
+            if 0 < p < 4:
+                add_pair(p - 1)
+            for k in range(len(mine)):
+                neighbour(spot("A", *mine[k]), mine[k][0], mine[k][1], (p, k) == (PAIRS - 2, len(mine) - 1))
+                if (p, k) == (3, 0):
+                    for g in range(PASSES):
+                        quantise(u + 4, g)
+        add_pair(PAIRS - 3)
 
         pair = (UNITS - 2, UNITS - 1)
-        unload(pair[0])
-        unload(pair[1])
+        scale_pair(PAIRS - 2)
+        add_pair(PAIRS - 2)
         summed = [keep.tile([P, PACK, P], F32, name="summed%d" % h, align_bytes=64) for h in range(HALVES)]
         for h in range(HALVES):
             nc.scalar.copy(out=summed[h][:], in_=acc[h][:].rearrange("v (p t) -> v t p", t=PACK))
-        early = banks.tile([P, 2, V], F32, name="early")
-        base = [banks.tile([P, 2, P], F32, name="base%d" % h, tag="acc%d" % h) for h in range(HALVES)]
-        for h in range(HALVES):
-            for t in range(2):
-                turn(early[:, t, h * P : (h + 1) * P], summed[h][:, t, :], (t, h) == (0, 0), False)
-                turn(base[h][:, t, :], summed[h][:, 2 + t, :], t == 0, False)
-        second_sums = keep.tile([P, HALVES, P], F32, name="second_sums", align_bytes=64)
-        nc.scalar.copy(out=second_sums[:], in_=mid_second[:])
-        for h in range(HALVES):
-            turn(early[:, 1, h * P : (h + 1) * P], second_sums[:, h, :], False, h == HALVES - 1)
+            for t in range(PACK):
+                turn_back(summed[h][:, t, :], t, h, (t, h) == (1, HALVES - 1))
         out_rows = out_0.rearrange("(p t) v -> p t v", t=PACK)
         sums = keep.tile([P, PACK, V], F32, name="sums", align_bytes=64)
-        nc.scalar.activation(out=sums[:, 0:2, :], in_=early[:], func=RELU)
-        nc.sync.dma_start(out=out_rows[:, 0:2, :], in_=sums[:, 0:2, :])
 
-        mid_first = banks.tile([P, HALVES, P], F32, name="mid_first")
+        mid_first = sbanks.tile([P, HALVES, P], F32, name="sbank")
         mid_last = [ybanks.tile([P, P], F32, name="ybank") for h in range(HALVES)]
         for d in range(D - 1):
             prod = prods.tile([P, V], F32, name="prod", align_bytes=64)
@@ -293,10 +360,12 @@ def tile_picked_zkp_three_po_kernel(tc, x_words, x_scales, w1, w2, w3, corr, off
         nc.scalar.copy(out=first_sums[:], in_=mid_first[:])
         last_sums = [keep.tile([P, P], F32, name="last_sums%d" % h, align_bytes=64) for h in range(HALVES)]
         for h in range(HALVES):
-            turn(base[h][:, 0, :], first_sums[:, h, :], False, False)
+            turn_back(first_sums[:, h, :], 2, h, False)
         for h in range(HALVES):
             nc.scalar.copy(out=last_sums[h][:], in_=mid_last[h][:])
-            turn(base[h][:, 1, :], last_sums[h][:], False, True)
+            turn_back(last_sums[h][:], 3, h, h == HALVES - 1)
+        nc.scalar.activation(out=sums[:, 0:2, :], in_=planes[0][:], func=RELU)
+        nc.sync.dma_start(out=out_rows[:, 0:2, :], in_=sums[:, 0:2, :])
         last_prods = keep.tile([P, 2, V], F32, name="last_prods", align_bytes=64)
         gather(last_prods[:, 0, :], pair[0], D - 1, 0, V)
         for h in range(HALVES):
@@ -308,7 +377,7 @@ def tile_picked_zkp_three_po_kernel(tc, x_words, x_scales, w1, w2, w3, corr, off
         late = keep.tile([P, 2, V], F32, name="late", align_bytes=64)
         halves = [slice(h * P, (h + 1) * P) for h in range(HALVES)]
         for cols in halves:
-            nc.vector.tensor_tensor(sums[:, 2:4, cols], last_prods[:, :, cols], base[cols.start // P][:], ADD)
+            nc.vector.tensor_tensor(sums[:, 2:4, cols], last_prods[:, :, cols], planes[1][:, :, cols], ADD)
         for cols in halves:
             nc.vector.tensor_scalar_max(
                 result_bf[:, cols, :].rearrange("p (c i) t -> p c t i", i=4), sums[:, :, cols].rearrange("p t (c i) -> p c t i", i=4), 0.0

@@ -253,7 +253,12 @@ def tile_picked_zkp_three_po_kernel(tc, x_words, x_scales, w1, w2, w3, corr, off
                 factor = near_cols[:, D * q + d, h : h + 1]
                 if u < DEALT_FROM:
                     rows = slice(c * P // PACK, (c + count) * P // PACK)
-                    nc.scalar.activation(scaled[key][:, h, :, rows], bank[:, h].rearrange("v (p t) -> v t p", t=PACK), COPY, scale=factor)
+                    nc.scalar.activation(
+                        scaled[key][:, h, :, rows].rearrange("v (a e) p -> v a p e", e=2),
+                        bank[:, h].rearrange("v (p a e) -> v a p e", a=2, e=2),
+                        COPY,
+                        scale=factor,
+                    )
                 else:
                     nc.scalar.activation(scaled[key][:, h, c : c + count, :].rearrange("v t p -> v (t p)"), bank[:, h], COPY, scale=factor)
 
@@ -335,7 +340,9 @@ def tile_picked_zkp_three_po_kernel(tc, x_words, x_scales, w1, w2, w3, corr, off
         add_pair(PAIRS - 2)
         summed = [keep.tile([P, PACK, P], F32, name="summed%d" % h, align_bytes=64) for h in range(HALVES)]
         for h in range(HALVES):
-            nc.scalar.copy(out=summed[h][:], in_=acc[h][:].rearrange("v (p t) -> v t p", t=PACK))
+            nc.scalar.copy(
+                out=summed[h][:].rearrange("v (a e) p -> v a p e", e=2), in_=acc[h][:].rearrange("v (p a e) -> v a p e", a=2, e=2)
+            )
             for t in range(PACK):
                 turn_back(summed[h][:, t, :], t, h, (t, h) == (1, HALVES - 1))
         out_rows = out_0.rearrange("(p t) v -> p t v", t=PACK)

@@ -27,21 +27,28 @@ UNITS = D * CHUNKS
 DEALT_FROM = (D - 1) * CHUNKS
 PAIRS = UNITS // 2
 EXTRA = ((1,), (3,), (4,), (6,), ())
+WEIGHED = (0, 5)
+LATE = ([], [], [(5, 2)], [], [])
 SCALAR_CASTS = ()
 HELD = {
     ("G", 1, 0): "raw2_1",
     ("G", 1, 1): "raw2_1",
-    ("A", 0, 1): "raw2_1",
     ("A", 1, 2): "rounded2_1",
-    ("G", 3, 0): "rounded4_1",
-    ("G", 3, 1): "rounded4_1",
+    ("G", 3, 0): "raw4_1",
+    ("G", 3, 1): "raw4_1",
     ("G", 5, 0): "rounded6_1",
     ("G", 4, 1): "rounded6_1",
-    ("A", 6, 2): "last_raw",
-    ("A", 7, 2): "last_raw",
-    ("A", 7, 1): "last_raw",
+    ("A", 6, 2): "rounded8_1",
+    ("A", 7, 2): "rounded8_1",
+    ("A", 7, 1): "rounded8_1",
     ("G", 7, 0): "rounded8_1",
     ("G", 6, 1): "rounded8_1",
+    ("M", 0, 1): "rounded2_1",
+    ("G", 5, 1): "rounded6_1",
+    ("M", 5, 1): "rounded8_1",
+    ("A", 5, 2): "rounded8_1",
+    ("A", 2, 1): "raw4_1",
+    ("A", 3, 2): "raw4_1",
 }
 
 
@@ -81,6 +88,13 @@ def tile_picked_zkp_three_po_kernel(tc, x_words, x_scales, w1, w2, w3, corr, off
             loaded[(u, g)] = tile
             return tile
 
+        def load_both(u):
+            q, c = divmod(u, CHUNKS)
+            loaded[u] = keep.tile([P, PASSES, PACK, 2 * P], F32, name="raw", tag="raw%d_1" % u, align_bytes=64)
+            for g in range(PASSES):
+                part = weights[q][g * 512 : (g + 1) * 512, c * P : (c + 2) * P]
+                nc.sync.dma_start(out=loaded[u][:, g], in_=part.rearrange("(p t) n -> p t n", t=PACK))
+
         def load_corr(*entries):
             tile = keep.tile([P, len(entries), V], F32, name="corr%d" % entries[0], align_bytes=64)
             step = entries[1] - entries[0] if len(entries) > 1 else 1
@@ -103,15 +117,15 @@ def tile_picked_zkp_three_po_kernel(tc, x_words, x_scales, w1, w2, w3, corr, off
         load_w(1, 1, 1)
         for d, pos in enumerate((pos1, pos2, pos3)):
             nc.sync.dma_start(pos_t[d][:], pos)
+        load_w(2, 0, 2)
+        load_corr(2)
+        load_w(2, 1, 2)
         corr_rows = keep.tile([P, P], F32, name="corr_rows", align_bytes=64)
         nc.sync.dma_start(out=corr_rows[:], in_=corr[0:8, 0:8, :].rearrange("i r (h v) -> i (r h) v", h=HALVES))
-        load_w(2, 0, 2)
-        load_corr(1, 2)
-        load_w(2, 1, 2)
+        load_corr(1)
         load_w(4, 0, 2)
         load_w(4, 1, 2)
-        load_w(6, 0, 2)
-        load_w(6, 1, 2)
+        load_both(6)
         load_corr(4, 5)
         whole = [load_w(DEALT_FROM, g, CHUNKS) for g in range(PASSES)]
         load_corr(6, 7, 8)
@@ -134,7 +148,8 @@ def tile_picked_zkp_three_po_kernel(tc, x_words, x_scales, w1, w2, w3, corr, off
 
         def cast(u, g):
             rounded[(u, g)] = keep.tile([P, P, PACK], BF16, name="rounded", tag="rounded%d_%d" % (u, g), align_bytes=64)
-            nc.scalar.copy(
+            copy = nc.vector.tensor_copy if (u, g) == (1, 1) else nc.scalar.copy
+            copy(
                 out=rounded[(u, g)][:].rearrange("p (c i) t -> p c t i", i=4), in_=raw[(u, g)].rearrange("p t (c i) -> p c t i", i=4)
             )
 
@@ -153,6 +168,22 @@ def tile_picked_zkp_three_po_kernel(tc, x_words, x_scales, w1, w2, w3, corr, off
                     in_=whole[g][:].rearrange("p t (m s) -> p m t s", s=PACK)[:, :, :, s : s + 2],
                 )
 
+        def cast_last(half):
+            if half == 0:
+                rounded[(UNITS - 2, 1)] = keep.tile([P, 2 * P, PACK], BF16, name="rounded_last", align_bytes=64)
+            rows = slice(half * P // 2, (half + 1) * P // 2)
+            nc.vector.tensor_copy(
+                out=rounded[(UNITS - 2, 1)][:].rearrange("p (s m) t -> p m t s", s=2)[:, rows],
+                in_=whole[1][:].rearrange("p t (m s) -> p m t s", s=PACK)[:, rows, :, 2:4],
+            )
+
+        def cast_unit(u, j):
+            rounded[(u, j)] = keep.tile([P, PASSES * P, PACK], BF16, name="rounded", tag="rounded%d_%d" % (u, j), align_bytes=64)
+            nc.vector.tensor_copy(
+                out=rounded[(u, j)][:].rearrange("p (g c i) t -> p g c t i", g=PASSES, i=4),
+                in_=loaded[u][:, :, :, j * P : (j + 1) * P].rearrange("p g t (c i) -> p g c t i", i=4),
+            )
+
         def quantise(u, g):
             width = rounded[(u, g)].shape[1]
             if (u, g) == (UNITS - 2, 0):
@@ -162,7 +193,8 @@ def tile_picked_zkp_three_po_kernel(tc, x_words, x_scales, w1, w2, w3, corr, off
             w_planes = keep.tile([P, width], U8, name="w_planes", tag="w_planes%d_%d" % (u, g), align_bytes=64)
             nc.vector.quantize_mx(out=w_codes[:].bitcast(FP8X4), scales=w_planes[:], in_=rounded[(u, g)][:].rearrange("p c t -> p (c t)"))
             for j in range(width // P):
-                codes[(u + j, g)] = (w_codes[:, j * P : (j + 1) * P], w_planes[:, j * P : (j + 1) * P])
+                key = (u + g, j) if u == 6 else (u + j, g)
+                codes[key] = (w_codes[:, j * P : (j + 1) * P], w_planes[:, j * P : (j + 1) * P])
 
         def one_pass(bank, u, g, part):
             w_codes, w_planes = codes[(u, g)]
@@ -221,6 +253,7 @@ def tile_picked_zkp_three_po_kernel(tc, x_words, x_scales, w1, w2, w3, corr, off
         planes_open = [False, False]
         sbank = {}
         scaled = {}
+        plain = {}
 
         def turn_back(tile, t, h, final):
             turn(planes[t // 2][:, t % 2, h * P : (h + 1) * P], tile, not planes_open[t // 2], final)
@@ -236,14 +269,25 @@ def tile_picked_zkp_three_po_kernel(tc, x_words, x_scales, w1, w2, w3, corr, off
             extra = EXTRA[pair]
             more = sbanks.tile([P, HALVES, len(extra), P], F32, name="sbank") if extra else None
             terms = [(2 * pair, 0), (2 * pair + 1, 0)] + [(u, 1) for u in extra]
-            if len(extra) == 2:
+            terms = terms + [(u, 1) for u in WEIGHED if u // 2 == pair]
+            if pair == 0:
                 terms = sorted(terms)
             for u, d in terms:
-                if d == 0:
+                if d == 1 and u in WEIGHED:
+                    plain[u] = spot("G", u, d)
+                    nc.scalar.activation(plain[u], y[u][:].indirect(pos_t[d][:]), COPY)
+                elif d == 0:
                     fetch(spot("G", u, d), u, d, both[:, :, u % 2, :], u % 2 == 0, u % 2 == 1)
                 else:
                     fetch(spot("G", u, d), u, d, more[:, :, u - extra[0], :], u == extra[0], u == extra[-1])
             sbank[pair] = (both, more)
+
+        def weigh_pair(pair):
+            for u in WEIGHED:
+                if u // 2 == pair:
+                    prod = spot("M", u, 1)
+                    nc.vector.tensor_tensor(prod, plain[u], near[D * (u // CHUNKS) + 1], MULT)
+                    add_wide(prod, u, False)
 
         def scale(key, bank, u, count, d):
             if key not in scaled:
@@ -278,6 +322,9 @@ def tile_picked_zkp_three_po_kernel(tc, x_words, x_scales, w1, w2, w3, corr, off
 
         def neighbour(prod, u, d, final):
             gather(prod, u, d, 0, V)
+            add_wide(prod, u, final)
+
+        def add_wide(prod, u, final):
             for h in range(HALVES):
                 block = prod[:, h * P : (h + 1) * P]
                 if u < DEALT_FROM:
@@ -303,15 +350,20 @@ def tile_picked_zkp_three_po_kernel(tc, x_words, x_scales, w1, w2, w3, corr, off
         for p in range(PAIRS - 1):
             u = 2 * p
             mine = [(u, 2), (u, 1), (u + 1, 2), (u + 1, 1)]
-            mine = [term for term in mine if term[1] == 2 or term[0] not in EXTRA[p]]
-            if p < 4:
+            mine = [term for term in mine if term not in LATE[p]] + LATE[p - 1]
+            mine = [term for term in mine if term[1] == 2 or term[0] not in EXTRA[p] + WEIGHED]
+            if p == 2:
+                cast_unit(u + 2, 0)
+                cast_unit(u + 2, 1)
+                quantise(u + 2, 0)
+            elif p < 4:
                 cast_pair(u + 2, 0)
                 if p == 3:
                     cast_pair(u + 4, 0)
                 cast_pair(u + 2, 1)
                 quantise(u + 2, 0)
                 if p == 3:
-                    cast_pair(u + 4, 1)
+                    cast_last(0)
             if p > 0:
                 unload(u)
             unload(u + 1)
@@ -319,6 +371,8 @@ def tile_picked_zkp_three_po_kernel(tc, x_words, x_scales, w1, w2, w3, corr, off
                 scale_pair(p - 1)
             if p < 4:
                 quantise(u + 2, 1)
+                if p == 3:
+                    cast_last(1)
                 for j in range(2):
                     multiply(u + 2 + j)
             if p == 4:
@@ -330,6 +384,10 @@ def tile_picked_zkp_three_po_kernel(tc, x_words, x_scales, w1, w2, w3, corr, off
                 add_pair(p - 1)
             for k in range(len(mine)):
                 neighbour(spot("A", *mine[k]), mine[k][0], mine[k][1], (p, k) == (PAIRS - 2, len(mine) - 1))
+                if k == 0 and p > 1:
+                    weigh_pair(p - 1)
+                if (p, k) == (0, len(mine) - 1):
+                    weigh_pair(0)
                 if (p, k) == (3, 0):
                     for g in range(PASSES):
                         quantise(u + 4, g)

@@ -18,38 +18,37 @@ ADD = mybir.AluOpType.add
 K, T, S, D, V, N = 1024, 1024, 512, 3, 256, 512
 P = 128
 PACK = 4
-PASSES = K // (P * PACK)
+PASS_ROWS = P * PACK
+PASSES = K // PASS_ROWS
 CHUNKS = N // P
 HALVES = V // P
+LINE = 4
 FLOPS = 2 * K * N * S * D
 
 UNITS = D * CHUNKS
 DEALT_FROM = (D - 1) * CHUNKS
 PAIRS = UNITS // 2
-EXTRA = ((1,), (3,), (4,), (6,), ())
+BY_UNIT = 6
+
+SCALED = ((1,), (3,), (4,), (6,), ())
 WEIGHED = (0, 5)
-LATE = ([], [], [(5, 2)], [], [])
-SCALAR_CASTS = ()
-HELD = {
-    ("G", 1, 0): "raw2_1",
-    ("G", 1, 1): "raw2_1",
-    ("A", 1, 2): "rounded2_1",
-    ("G", 3, 0): "raw4_1",
-    ("G", 3, 1): "raw4_1",
-    ("G", 5, 0): "rounded6_1",
-    ("G", 4, 1): "rounded6_1",
-    ("A", 6, 2): "rounded8_1",
-    ("A", 7, 2): "rounded8_1",
-    ("A", 7, 1): "rounded8_1",
-    ("G", 7, 0): "rounded8_1",
-    ("G", 6, 1): "rounded8_1",
-    ("M", 0, 1): "rounded2_1",
-    ("G", 5, 1): "rounded6_1",
-    ("M", 5, 1): "rounded8_1",
-    ("A", 5, 2): "rounded8_1",
-    ("A", 2, 1): "raw4_1",
-    ("A", 3, 2): "raw4_1",
+PUT_OFF = (5, 2)
+
+WAITS = {
+    "raw2_1": [("fetch", 1, 0), ("fetch", 1, 1), ("fused", 1, 2), ("weigh", 0, 1)],
+    "raw4_1": [("fetch", 3, 0), ("fetch", 3, 1), ("fused", 2, 1), ("fused", 3, 2)],
+    "rounded6_1": [("fetch", 5, 0), ("fetch", 4, 1), ("fetch", 5, 1)],
+    "rounded8_1": [
+        ("fused", 6, 2),
+        ("fused", 7, 2),
+        ("fused", 7, 1),
+        ("fetch", 7, 0),
+        ("fetch", 6, 1),
+        ("weigh", 5, 1),
+        ("fused", 5, 2),
+    ],
 }
+HELD_CODES_OFFSET = PACK * N * 4 - 2 * P * 4
 
 
 def tile_picked_zkp_three_po_kernel(tc, x_words, x_scales, w1, w2, w3, corr, offs, pos1, pos2, pos3, out_0, out_1, out_2):
@@ -69,38 +68,34 @@ def tile_picked_zkp_three_po_kernel(tc, x_words, x_scales, w1, w2, w3, corr, off
         x_all = [keep.tile([P, T], I32, name="x_all%d" % g, align_bytes=64) for g in range(PASSES)]
         xs_all = keep.tile([P, T], U8, name="xs_all", align_bytes=64)
         near = {}
-        raw = {}
         loaded = {}
 
         def load_x(g):
             nc.sync.dma_start(out=x_all[g][:], in_=x_words[g].rearrange("p n t -> p (n t)").bitcast(I32))
 
-        def load_w(u, g, count):
+        def weight_rows(u, g, count):
             q, c = divmod(u, CHUNKS)
+            part = weights[q][g * PASS_ROWS : (g + 1) * PASS_ROWS, c * P : (c + count) * P]
+            return part.rearrange("(p t) n -> p t n", t=PACK)
+
+        def load_w(u, g, count):
             if (u, g) == (DEALT_FROM, 1):
                 tile = placed.tile([P, PACK, count * P], F32, name="last_raw", align_bytes=64, offset=0)
             else:
                 tile = keep.tile([P, PACK, count * P], F32, name="raw", tag="raw%d_%d" % (u, g), align_bytes=64)
-            part = weights[q][g * 512 : (g + 1) * 512, c * P : (c + count) * P]
-            nc.sync.dma_start(out=tile[:], in_=part.rearrange("(p t) n -> p t n", t=PACK))
-            for j in range(count):
-                raw[(u + j, g)] = tile[:, :, j * P : (j + 1) * P]
+            nc.sync.dma_start(out=tile[:], in_=weight_rows(u, g, count))
             loaded[(u, g)] = tile
-            return tile
 
-        def load_both(u):
-            q, c = divmod(u, CHUNKS)
+        def load_both_passes(u):
             loaded[u] = keep.tile([P, PASSES, PACK, 2 * P], F32, name="raw", tag="raw%d_1" % u, align_bytes=64)
             for g in range(PASSES):
-                part = weights[q][g * 512 : (g + 1) * 512, c * P : (c + 2) * P]
-                nc.sync.dma_start(out=loaded[u][:, g], in_=part.rearrange("(p t) n -> p t n", t=PACK))
+                nc.sync.dma_start(out=loaded[u][:, g], in_=weight_rows(u, g, 2))
 
-        def load_corr(*entries):
-            tile = keep.tile([P, len(entries), V], F32, name="corr%d" % entries[0], align_bytes=64)
-            step = entries[1] - entries[0] if len(entries) > 1 else 1
-            nc.sync.dma_start(out=tile[:], in_=corr[entries[0] : entries[-1] + 1 : step].rearrange("d p v -> p d v"))
-            for j, i in enumerate(entries):
-                near[i] = tile[:, j, :]
+        def load_corr(lo, hi):
+            tile = keep.tile([P, hi - lo, V], F32, name="corr%d" % lo, align_bytes=64)
+            nc.sync.dma_start(out=tile[:], in_=corr[lo:hi].rearrange("d p v -> p d v"))
+            for i in range(lo, hi):
+                near[i] = tile[:, i - lo, :]
 
         nc.gpsimd.memset(xs_all[:].bitcast(I32), 0)
         nc.sync.dma_start(offs_t[:], offs)
@@ -118,17 +113,18 @@ def tile_picked_zkp_three_po_kernel(tc, x_words, x_scales, w1, w2, w3, corr, off
         for d, pos in enumerate((pos1, pos2, pos3)):
             nc.sync.dma_start(pos_t[d][:], pos)
         load_w(2, 0, 2)
-        load_corr(2)
+        load_corr(2, 3)
         load_w(2, 1, 2)
         corr_rows = keep.tile([P, P], F32, name="corr_rows", align_bytes=64)
         nc.sync.dma_start(out=corr_rows[:], in_=corr[0:8, 0:8, :].rearrange("i r (h v) -> i (r h) v", h=HALVES))
-        load_corr(1)
+        load_corr(1, 2)
         load_w(4, 0, 2)
         load_w(4, 1, 2)
-        load_both(6)
-        load_corr(4, 5)
-        whole = [load_w(DEALT_FROM, g, CHUNKS) for g in range(PASSES)]
-        load_corr(6, 7, 8)
+        load_both_passes(BY_UNIT)
+        load_corr(4, 6)
+        for g in range(PASSES):
+            load_w(DEALT_FROM, g, CHUNKS)
+        load_corr(6, 9)
 
         ident = keep.tile([P, P], F32, name="ident")
         make_identity(nc, ident[:])
@@ -146,64 +142,60 @@ def tile_picked_zkp_three_po_kernel(tc, x_words, x_scales, w1, w2, w3, corr, off
         ybank = {}
         y = {}
 
-        def cast(u, g):
-            rounded[(u, g)] = keep.tile([P, P, PACK], BF16, name="rounded", tag="rounded%d_%d" % (u, g), align_bytes=64)
-            copy = nc.vector.tensor_copy if (u, g) == (1, 1) else nc.scalar.copy
+        def round_pass(copy, u, g, count):
+            rounded[(u, g)] = keep.tile([P, count * P, PACK], BF16, name="rounded", tag="rounded%d_%d" % (u, g), align_bytes=64)
             copy(
-                out=rounded[(u, g)][:].rearrange("p (c i) t -> p c t i", i=4), in_=raw[(u, g)].rearrange("p t (c i) -> p c t i", i=4)
+                out=rounded[(u, g)][:].rearrange("p (c i) t -> p c t i", i=LINE),
+                in_=loaded[(u, g)][:].rearrange("p t (c i) -> p c t i", i=LINE),
             )
 
-        def cast_pair(u, g):
-            both = keep.tile([P, 2 * P, PACK], BF16, name="rounded", tag="rounded%d_%d" % (u, g), align_bytes=64)
-            rounded[(u, g)] = both
+        def dealt_views(u, g):
             s = u - DEALT_FROM
-            copy = nc.scalar.copy if (u, g) in SCALAR_CASTS else nc.vector.tensor_copy
-            if s < 0:
-                copy(
-                    out=both[:].rearrange("p (c i) t -> p c t i", i=4), in_=loaded[(u, g)][:].rearrange("p t (c i) -> p c t i", i=4)
-                )
-            else:
-                copy(
-                    out=both[:].rearrange("p (s m) t -> p m t s", s=2),
-                    in_=whole[g][:].rearrange("p t (m s) -> p m t s", s=PACK)[:, :, :, s : s + 2],
-                )
+            target = rounded[(u, g)][:].rearrange("p (s m) t -> p m t s", s=2)
+            source = loaded[(DEALT_FROM, g)][:].rearrange("p t (m s) -> p m t s", s=PACK)[:, :, :, s : s + 2]
+            return target, source
 
-        def cast_last(half):
+        def round_dealt(u, g):
+            rounded[(u, g)] = keep.tile([P, 2 * P, PACK], BF16, name="rounded", tag="rounded%d_%d" % (u, g), align_bytes=64)
+            target, source = dealt_views(u, g)
+            nc.vector.tensor_copy(out=target, in_=source)
+
+        def round_last(half):
             if half == 0:
                 rounded[(UNITS - 2, 1)] = keep.tile([P, 2 * P, PACK], BF16, name="rounded_last", align_bytes=64)
             rows = slice(half * P // 2, (half + 1) * P // 2)
-            nc.vector.tensor_copy(
-                out=rounded[(UNITS - 2, 1)][:].rearrange("p (s m) t -> p m t s", s=2)[:, rows],
-                in_=whole[1][:].rearrange("p t (m s) -> p m t s", s=PACK)[:, rows, :, 2:4],
-            )
+            target, source = dealt_views(UNITS - 2, 1)
+            nc.vector.tensor_copy(out=target[:, rows], in_=source[:, rows])
 
-        def cast_unit(u, j):
+        def round_unit(u, j):
             rounded[(u, j)] = keep.tile([P, PASSES * P, PACK], BF16, name="rounded", tag="rounded%d_%d" % (u, j), align_bytes=64)
             nc.vector.tensor_copy(
-                out=rounded[(u, j)][:].rearrange("p (g c i) t -> p g c t i", g=PASSES, i=4),
-                in_=loaded[u][:, :, :, j * P : (j + 1) * P].rearrange("p g t (c i) -> p g c t i", i=4),
+                out=rounded[(u, j)][:].rearrange("p (g c i) t -> p g c t i", g=PASSES, i=LINE),
+                in_=loaded[u][:, :, :, j * P : (j + 1) * P].rearrange("p g t (c i) -> p g c t i", i=LINE),
             )
 
-        def quantise(u, g):
-            width = rounded[(u, g)].shape[1]
-            if (u, g) == (UNITS - 2, 0):
-                w_codes = placed.tile([P, width], I32, name="held_codes", align_bytes=64, offset=7 * V * 4)
+        def quantise(u, part):
+            width = rounded[(u, part)].shape[1]
+            if (u, part) == (UNITS - 2, 0):
+                w_codes = placed.tile([P, width], I32, name="held_codes", align_bytes=64, offset=HELD_CODES_OFFSET)
             else:
-                w_codes = keep.tile([P, width], I32, name="w_codes", tag="w_codes%d_%d" % (u, g), align_bytes=64)
-            w_planes = keep.tile([P, width], U8, name="w_planes", tag="w_planes%d_%d" % (u, g), align_bytes=64)
-            nc.vector.quantize_mx(out=w_codes[:].bitcast(FP8X4), scales=w_planes[:], in_=rounded[(u, g)][:].rearrange("p c t -> p (c t)"))
+                w_codes = keep.tile([P, width], I32, name="w_codes", tag="w_codes%d_%d" % (u, part), align_bytes=64)
+            w_planes = keep.tile([P, width], U8, name="w_planes", tag="w_planes%d_%d" % (u, part), align_bytes=64)
+            nc.vector.quantize_mx(
+                out=w_codes[:].bitcast(FP8X4), scales=w_planes[:], in_=rounded[(u, part)][:].rearrange("p c t -> p (c t)")
+            )
             for j in range(width // P):
-                key = (u + g, j) if u == 6 else (u + j, g)
+                key = (u + part, j) if u == BY_UNIT else (u + j, part)
                 codes[key] = (w_codes[:, j * P : (j + 1) * P], w_planes[:, j * P : (j + 1) * P])
 
-        def one_pass(bank, u, g, part):
+        def one_pass(bank, u, g, points):
             w_codes, w_planes = codes[(u, g)]
             nc.tensor.matmul_mx(
                 out=bank,
                 lhsT=w_codes.bitcast(FP8X4),
                 lhsT_scale=w_planes,
-                rhs=x_codes[g][:, part].bitcast(FP8X4),
-                rhs_scale=x_planes[4 * g : P, part],
+                rhs=x_codes[g][:, points].bitcast(FP8X4),
+                rhs_scale=x_planes[4 * g : P, points],
                 start=(g == 0),
                 stop=(g == PASSES - 1),
             )
@@ -217,27 +209,29 @@ def tile_picked_zkp_three_po_kernel(tc, x_words, x_scales, w1, w2, w3, corr, off
             y[u] = keep.tile([P, S], F32, name="y", tag="y%d" % u, align_bytes=64)
             nc.scalar.copy(out=y[u][:], in_=ybank[u][:])
 
+        def entry(u, d):
+            return D * (u // CHUNKS) + d
+
         def gather(prod, u, d, lo, hi):
-            nc.vector.tensor_tensor(prod, y[u][:].indirect(pos_t[d][:, lo // 16 : hi // 16]), near[D * (u // CHUNKS) + d][:, lo:hi], MULT)
+            nc.vector.tensor_tensor(prod, y[u][:].indirect(pos_t[d][:, lo // 16 : hi // 16]), near[entry(u, d)][:, lo:hi], MULT)
 
         for g in range(PASSES):
-            cast(0, g)
+            round_pass(nc.scalar.copy, 0, g, 1)
             quantise(0, g)
         x_codes.append(keep.tile([P, S], I32, name="x_codes1", tag="raw0_1", align_bytes=64))
-        first = [sbanks.tile([P, S // 2], F32, name="sbank") for j in range(2)]
+        point_halves = [slice(j * S // 2, (j + 1) * S // 2) for j in range(2)]
+        first_product = [sbanks.tile([P, S // 2], F32, name="sbank") for j in range(2)]
         for g in range(PASSES):
-            for j in range(2):
-                part = slice(j * S // 2, (j + 1) * S // 2)
+            for j, points in enumerate(point_halves):
                 if g == PASSES - 1:
-                    nc.vector.tensor_copy(
-                        x_codes[g][:, part].bitcast(U32), x_all[g][:].bitcast(U32).indirect(offs_t[:, 16 * j : 16 * j + 16])
-                    )
-                one_pass(first[j][:], 0, g, part)
-        cast(1, 0)
-        cast(1, 1)
+                    half_list = offs_t[:, points.start // 16 : points.stop // 16]
+                    nc.vector.tensor_copy(x_codes[g][:, points].bitcast(U32), x_all[g][:].bitcast(U32).indirect(half_list))
+                one_pass(first_product[j][:], 0, g, points)
+        round_pass(nc.scalar.copy, 1, 0, 1)
+        round_pass(nc.vector.tensor_copy, 1, 1, 1)
         y[0] = keep.tile([P, S], F32, name="y", tag="y0", align_bytes=64)
-        for j in range(2):
-            nc.scalar.copy(out=y[0][:, j * S // 2 : (j + 1) * S // 2], in_=first[j][:])
+        for j, points in enumerate(point_halves):
+            nc.scalar.copy(out=y[0][:, points], in_=first_product[j][:])
         quantise(1, 0)
         quantise(1, 1)
         multiply(1)
@@ -247,210 +241,210 @@ def tile_picked_zkp_three_po_kernel(tc, x_words, x_scales, w1, w2, w3, corr, off
         near_cols = keep.tile([P, 8, HALVES], F32, name="near_cols", align_bytes=64)
         nc.scalar.copy(out=near_cols[:], in_=rows_turned[:].rearrange("v (i r h) -> v i r h", i=8, h=HALVES)[:, :, 0, :])
 
-        acc = [banks.tile([P, N], F32, name="acc%d" % h, tag="acc%d" % h) for h in range(HALVES)]
+        wide = [banks.tile([P, N], F32, name="acc%d" % h, tag="acc%d" % h) for h in range(HALVES)]
         planes = [banks.tile([P, 2, V], F32, name="planes%d" % a, tag="planes%d" % a) for a in range(2)]
-        acc_open = [False]
-        planes_open = [False, False]
-        sbank = {}
+        opened = set()
+        fetched_banks = {}
         scaled = {}
         plain = {}
+        waiting = {}
+
+        def opens(group):
+            fresh = group not in opened
+            opened.add(group)
+            return fresh
+
+        def buffer_for(*term):
+            for tag, terms in WAITS.items():
+                if term in terms:
+                    if tag not in waiting:
+                        waiting[tag] = keep.tile([P, len(terms), V], F32, name="later", tag=tag, align_bytes=64)
+                    return waiting[tag][:, terms.index(term), :]
+            return prods.tile([P, V], F32, name="prod", align_bytes=64)[:]
 
         def turn_back(tile, t, h, final):
-            turn(planes[t // 2][:, t % 2, h * P : (h + 1) * P], tile, not planes_open[t // 2], final)
-            planes_open[t // 2] = True
+            turn(planes[t // 2][:, t % 2, h * P : (h + 1) * P], tile, opens(("planes", t // 2)), final)
 
-        def fetch(plain, u, d, bank, first, final):
-            nc.scalar.activation(plain[:], y[u][:].indirect(pos_t[d][:]), COPY)
+        def fetch(u, d):
+            target = buffer_for("fetch", u, d)
+            nc.scalar.activation(target, y[u][:].indirect(pos_t[d][:]), COPY)
+            return target
+
+        def fetch_and_turn(u, d, bank, first, final):
+            values = fetch(u, d)
             for h in range(HALVES):
-                turn(bank[:, h, :], plain[:, h * P : (h + 1) * P], first and h == 0, final and h == HALVES - 1)
+                turn(bank[:, h, :], values[:, h * P : (h + 1) * P], first and h == 0, final and h == HALVES - 1)
 
         def fetch_pair(pair):
-            both = sbanks.tile([P, HALVES, 2, P], F32, name="sbank")
-            extra = EXTRA[pair]
-            more = sbanks.tile([P, HALVES, len(extra), P], F32, name="sbank") if extra else None
+            firsts = sbanks.tile([P, HALVES, 2, P], F32, name="sbank")
+            extra = SCALED[pair]
+            seconds = sbanks.tile([P, HALVES, len(extra), P], F32, name="sbank") if extra else None
             terms = [(2 * pair, 0), (2 * pair + 1, 0)] + [(u, 1) for u in extra]
             terms = terms + [(u, 1) for u in WEIGHED if u // 2 == pair]
             if pair == 0:
                 terms = sorted(terms)
             for u, d in terms:
-                if d == 1 and u in WEIGHED:
-                    plain[u] = spot("G", u, d)
-                    nc.scalar.activation(plain[u], y[u][:].indirect(pos_t[d][:]), COPY)
-                elif d == 0:
-                    fetch(spot("G", u, d), u, d, both[:, :, u % 2, :], u % 2 == 0, u % 2 == 1)
+                if d == 0:
+                    fetch_and_turn(u, d, firsts[:, :, u % 2, :], u % 2 == 0, u % 2 == 1)
+                elif u in WEIGHED:
+                    plain[u] = fetch(u, d)
                 else:
-                    fetch(spot("G", u, d), u, d, more[:, :, u - extra[0], :], u == extra[0], u == extra[-1])
-            sbank[pair] = (both, more)
-
-        def weigh_pair(pair):
-            for u in WEIGHED:
-                if u // 2 == pair:
-                    prod = spot("M", u, 1)
-                    nc.vector.tensor_tensor(prod, plain[u], near[D * (u // CHUNKS) + 1], MULT)
-                    add_wide(prod, u, False)
-
-        def scale(key, bank, u, count, d):
-            if key not in scaled:
-                scaled[key] = keep.tile([P, HALVES, PACK, P], F32, name="scaled%s" % key, align_bytes=64)
-            q, c = divmod(u, CHUNKS)
-            for h in range(HALVES):
-                factor = near_cols[:, D * q + d, h : h + 1]
-                if u < DEALT_FROM:
-                    rows = slice(c * P // PACK, (c + count) * P // PACK)
-                    nc.scalar.activation(
-                        scaled[key][:, h, :, rows].rearrange("v (a e) p -> v a p e", e=2),
-                        bank[:, h].rearrange("v (p a e) -> v a p e", a=2, e=2),
-                        COPY,
-                        scale=factor,
-                    )
-                else:
-                    nc.scalar.activation(scaled[key][:, h, c : c + count, :].rearrange("v t p -> v (t p)"), bank[:, h], COPY, scale=factor)
-
-        def scale_pair(pair):
-            both, more = sbank[pair]
-            scale("a%d" % (pair // 2), both[:].rearrange("v h j m -> v h (j m)"), 2 * pair, 2, 0)
-            if more is not None:
-                scale("b%d" % (pair // 4), more[:].rearrange("v h j m -> v h (j m)"), EXTRA[pair][0], len(EXTRA[pair]), 1)
-
-        def add_pair(pair):
-            keys = ["a%d" % (pair // 2), "b%d" % (pair // 4)]
-            counts = [(0, 0), (PACK, 0), (0, 0), (PACK, PACK), (2, len(EXTRA[4]))][pair]
-            for key, count in zip(keys, counts):
-                for h in range(HALVES):
-                    for t in range(count):
-                        turn_back(scaled[key][:, h, t, :], t, h, False)
-
-        def neighbour(prod, u, d, final):
-            gather(prod, u, d, 0, V)
-            add_wide(prod, u, final)
+                    fetch_and_turn(u, d, seconds[:, :, 0, :], True, True)
+            fetched_banks[pair] = (firsts, seconds)
 
         def add_wide(prod, u, final):
             for h in range(HALVES):
                 block = prod[:, h * P : (h + 1) * P]
                 if u < DEALT_FROM:
                     c = u % CHUNKS
-                    turn(acc[h][:, c * P : (c + 1) * P], block, not acc_open[0], False)
+                    turn(wide[h][:, c * P : (c + 1) * P], block, opens(("wide", h)), False)
                 else:
-                    turn(acc[h][:].rearrange("v (p t) -> v t p", t=PACK)[:, u - DEALT_FROM, :], block, False, final)
-            acc_open[0] = True
+                    turn(wide[h][:].rearrange("v (p t) -> v t p", t=PACK)[:, u - DEALT_FROM, :], block, False, final)
 
-        later = {}
+        def weigh_pair(pair):
+            for u in WEIGHED:
+                if u // 2 == pair:
+                    prod = buffer_for("weigh", u, 1)
+                    nc.vector.tensor_tensor(prod, plain[u], near[entry(u, 1)], MULT)
+                    add_wide(prod, u, False)
 
-        def spot(*key):
-            if key not in HELD:
-                return prods.tile([P, V], F32, name="prod", align_bytes=64)[:]
-            tag = HELD[key]
-            mates = [other for other in HELD if HELD[other] == tag]
-            if tag == "last_raw":
-                return placed.tile([P, V], F32, name="later%d" % mates.index(key), align_bytes=64, offset=mates.index(key) * V * 4)[:]
-            if tag not in later:
-                later[tag] = keep.tile([P, len(mates), V], F32, name="later", tag=tag, align_bytes=64)
-            return later[tag][:, mates.index(key), :]
+        def by_plane(target, source):
+            return target.rearrange("v (a e) p -> v a p e", e=2), source.rearrange("v (p a e) -> v a p e", a=2, e=2)
 
+        def scale(key, bank, u, count, d):
+            if key not in scaled:
+                scaled[key] = keep.tile([P, HALVES, PACK, P], F32, name="scaled%s" % key, align_bytes=64)
+            c = u % CHUNKS
+            for h in range(HALVES):
+                if u < DEALT_FROM:
+                    rows = slice(c * P // PACK, (c + count) * P // PACK)
+                    target, source = by_plane(scaled[key][:, h, :, rows], bank[:, h])
+                else:
+                    target, source = scaled[key][:, h, c : c + count, :].rearrange("v t p -> v (t p)"), bank[:, h]
+                nc.scalar.activation(target, source, COPY, scale=near_cols[:, entry(u, d), h : h + 1])
+
+        def scale_pair(pair):
+            firsts, seconds = fetched_banks[pair]
+            scale("a%d" % (pair // 2), firsts[:].rearrange("v h j m -> v h (j m)"), 2 * pair, 2, 0)
+            if SCALED[pair]:
+                scale("b0", seconds[:].rearrange("v h j m -> v h (j m)"), SCALED[pair][0], 1, 1)
+
+        def turn_tile_back(key, count):
+            for h in range(HALVES):
+                for t in range(count):
+                    turn_back(scaled[key][:, h, t, :], t, h, False)
+
+        last_step = PAIRS - 2
         for p in range(PAIRS - 1):
             u = 2 * p
-            mine = [(u, 2), (u, 1), (u + 1, 2), (u + 1, 1)]
-            mine = [term for term in mine if term not in LATE[p]] + LATE[p - 1]
-            mine = [term for term in mine if term[1] == 2 or term[0] not in EXTRA[p] + WEIGHED]
-            if p == 2:
-                cast_unit(u + 2, 0)
-                cast_unit(u + 2, 1)
-                quantise(u + 2, 0)
-            elif p < 4:
-                cast_pair(u + 2, 0)
-                if p == 3:
-                    cast_pair(u + 4, 0)
-                cast_pair(u + 2, 1)
-                quantise(u + 2, 0)
-                if p == 3:
-                    cast_last(0)
+            ahead = u + 2
+            fused = [term for term in [(u, 2), (u, 1), (u + 1, 2), (u + 1, 1)] if term != PUT_OFF]
+            fused = [term for term in fused if term[1] == 2 or term[0] not in SCALED[p] + WEIGHED]
+            if p == PUT_OFF[0] // 2 + 1:
+                fused.append(PUT_OFF)
+            if ahead == BY_UNIT:
+                round_unit(ahead, 0)
+                round_unit(ahead, 1)
+            elif ahead < DEALT_FROM:
+                round_pass(nc.vector.tensor_copy, ahead, 0, 2)
+                round_pass(nc.vector.tensor_copy, ahead, 1, 2)
+            elif ahead == DEALT_FROM:
+                round_dealt(ahead, 0)
+                round_dealt(ahead + 2, 0)
+                round_dealt(ahead, 1)
+            if p < last_step:
+                quantise(ahead, 0)
+            if ahead == DEALT_FROM:
+                round_last(0)
             if p > 0:
                 unload(u)
             unload(u + 1)
             if p > 0:
                 scale_pair(p - 1)
-            if p < 4:
-                quantise(u + 2, 1)
-                if p == 3:
-                    cast_last(1)
-                for j in range(2):
-                    multiply(u + 2 + j)
-            if p == 4:
-                for j in range(2):
-                    multiply(u + 2 + j)
-                    unload(u + 2 + j)
+            if p < last_step:
+                quantise(ahead, 1)
+            if ahead == DEALT_FROM:
+                round_last(1)
+            for j in range(2):
+                multiply(ahead + j)
+                if p == last_step:
+                    unload(ahead + j)
             fetch_pair(p)
-            if 0 < p < 4:
-                add_pair(p - 1)
-            for k in range(len(mine)):
-                neighbour(spot("A", *mine[k]), mine[k][0], mine[k][1], (p, k) == (PAIRS - 2, len(mine) - 1))
+            if p == CHUNKS // 2:
+                turn_tile_back("a0", PACK)
+            for k, (unit, d) in enumerate(fused):
+                prod = buffer_for("fused", unit, d)
+                gather(prod, unit, d, 0, V)
+                add_wide(prod, unit, (p, k) == (last_step, len(fused) - 1))
                 if k == 0 and p > 1:
                     weigh_pair(p - 1)
-                if (p, k) == (0, len(mine) - 1):
+                if (p, k) == (0, len(fused) - 1):
                     weigh_pair(0)
-                if (p, k) == (3, 0):
+                if k == 0 and ahead == DEALT_FROM:
                     for g in range(PASSES):
-                        quantise(u + 4, g)
-        add_pair(PAIRS - 3)
+                        quantise(ahead + 2, g)
+        turn_tile_back("a1", PACK)
+        turn_tile_back("b0", PACK)
 
-        pair = (UNITS - 2, UNITS - 1)
-        scale_pair(PAIRS - 2)
-        add_pair(PAIRS - 2)
+        scale_pair(last_step)
+        turn_tile_back("a2", 2)
         summed = [keep.tile([P, PACK, P], F32, name="summed%d" % h, align_bytes=64) for h in range(HALVES)]
         for h in range(HALVES):
-            nc.scalar.copy(
-                out=summed[h][:].rearrange("v (a e) p -> v a p e", e=2), in_=acc[h][:].rearrange("v (p a e) -> v a p e", a=2, e=2)
-            )
+            target, source = by_plane(summed[h][:], wide[h][:])
+            nc.scalar.copy(out=target, in_=source)
             for t in range(PACK):
                 turn_back(summed[h][:, t, :], t, h, (t, h) == (1, HALVES - 1))
         out_rows = out_0.rearrange("(p t) v -> p t v", t=PACK)
         sums = keep.tile([P, PACK, V], F32, name="sums", align_bytes=64)
 
-        mid_first = sbanks.tile([P, HALVES, P], F32, name="sbank")
-        mid_last = [ybanks.tile([P, P], F32, name="ybank") for h in range(HALVES)]
+        unit_a, unit_b = UNITS - 2, UNITS - 1
+        bank_a = sbanks.tile([P, HALVES, P], F32, name="sbank")
+        bank_b = [ybanks.tile([P, P], F32, name="ybank") for h in range(HALVES)]
         for d in range(D - 1):
             prod = prods.tile([P, V], F32, name="prod", align_bytes=64)
-            gather(prod[:], pair[0], d, 0, V)
+            gather(prod[:], unit_a, d, 0, V)
             for h in range(HALVES):
-                turn(mid_first[:, h, :], prod[:, h * P : (h + 1) * P], (d, h) == (0, 0), (d, h) == (D - 2, HALVES - 1))
+                turn(bank_a[:, h, :], prod[:, h * P : (h + 1) * P], (d, h) == (0, 0), (d, h) == (D - 2, HALVES - 1))
         prod = keep.tile([P, V], F32, name="prod", tag="last_prods", align_bytes=64)
-        gather(prod[:], pair[1], 0, 0, V)
+        gather(prod[:], unit_b, 0, 0, V)
         for h in range(HALVES):
-            turn(mid_last[h][:], prod[:, h * P : (h + 1) * P], True, False)
+            turn(bank_b[h][:], prod[:, h * P : (h + 1) * P], True, False)
         for h in range(HALVES):
             prod = prods.tile([P, P], F32, name="prod", align_bytes=64)
-            gather(prod[:], pair[1], 1, h * P, (h + 1) * P)
-            turn(mid_last[h][:], prod[:], False, True)
-        first_sums = keep.tile([P, HALVES, P], F32, name="first_sums", align_bytes=64)
-        nc.scalar.copy(out=first_sums[:], in_=mid_first[:])
-        last_sums = [keep.tile([P, P], F32, name="last_sums%d" % h, align_bytes=64) for h in range(HALVES)]
+            gather(prod[:], unit_b, 1, h * P, (h + 1) * P)
+            turn(bank_b[h][:], prod[:], False, True)
+        sums_a = keep.tile([P, HALVES, P], F32, name="first_sums", align_bytes=64)
+        nc.scalar.copy(out=sums_a[:], in_=bank_a[:])
+        sums_b = [keep.tile([P, P], F32, name="last_sums%d" % h, align_bytes=64) for h in range(HALVES)]
         for h in range(HALVES):
-            turn_back(first_sums[:, h, :], 2, h, False)
+            turn_back(sums_a[:, h, :], 2, h, False)
         for h in range(HALVES):
-            nc.scalar.copy(out=last_sums[h][:], in_=mid_last[h][:])
-            turn_back(last_sums[h][:], 3, h, h == HALVES - 1)
+            nc.scalar.copy(out=sums_b[h][:], in_=bank_b[h][:])
+            turn_back(sums_b[h][:], 3, h, h == HALVES - 1)
         nc.scalar.activation(out=sums[:, 0:2, :], in_=planes[0][:], func=RELU)
         nc.sync.dma_start(out=out_rows[:, 0:2, :], in_=sums[:, 0:2, :])
         last_prods = keep.tile([P, 2, V], F32, name="last_prods", align_bytes=64)
-        gather(last_prods[:, 0, :], pair[0], D - 1, 0, V)
+        gather(last_prods[:, 0, :], unit_a, D - 1, 0, V)
         for h in range(HALVES):
-            gather(last_prods[:, 1, h * P : (h + 1) * P], pair[1], D - 1, h * P, (h + 1) * P)
+            gather(last_prods[:, 1, h * P : (h + 1) * P], unit_b, D - 1, h * P, (h + 1) * P)
 
         out_words = keep.tile([P, V], I32, name="out_words", align_bytes=64)
         out_planes = keep.tile([P, V], U8, name="out_planes", align_bytes=64)
         result_bf = keep.tile([P, V, PACK], BF16, name="result_bf", align_bytes=64)
         late = keep.tile([P, 2, V], F32, name="late", align_bytes=64)
-        halves = [slice(h * P, (h + 1) * P) for h in range(HALVES)]
-        for cols in halves:
+        centre_halves = [slice(h * P, (h + 1) * P) for h in range(HALVES)]
+        for cols in centre_halves:
             nc.vector.tensor_tensor(sums[:, 2:4, cols], last_prods[:, :, cols], planes[1][:, :, cols], ADD)
-        for cols in halves:
+        for cols in centre_halves:
             nc.vector.tensor_scalar_max(
-                result_bf[:, cols, :].rearrange("p (c i) t -> p c t i", i=4), sums[:, :, cols].rearrange("p t (c i) -> p c t i", i=4), 0.0
+                result_bf[:, cols, :].rearrange("p (c i) t -> p c t i", i=LINE),
+                sums[:, :, cols].rearrange("p t (c i) -> p c t i", i=LINE),
+                0.0,
             )
-        for cols in halves:
+        for cols in centre_halves:
             nc.scalar.activation(out=late[:, :, cols], in_=sums[:, 2:4, cols], func=RELU)
             nc.sync.dma_start(out=out_rows[:, 2:4, cols], in_=late[:, :, cols])
-        for cols in halves:
+        for cols in centre_halves:
             nc.vector.quantize_mx(
                 out=out_words[:, cols].bitcast(FP8X4), scales=out_planes[:, cols], in_=result_bf[:, cols, :].rearrange("p c t -> p (c t)")
             )

@@ -35,7 +35,7 @@ WEIGHED = (0, 5)
 PUT_OFF = (5, 2)
 
 WAITS = {
-    "raw2_1": [("fetch", 1, 0), ("fetch", 1, 1), ("fused", 1, 2), ("weigh", 0, 1)],
+    "raw2_1": [("fetch", 1, 0), ("fetch", 1, 1), ("fused", 1, 2)],
     "raw4_1": [("fetch", 3, 0), ("fetch", 3, 1), ("fused", 2, 1), ("fused", 3, 2)],
     "rounded6_1": [("fetch", 5, 0), ("fetch", 4, 1), ("fetch", 5, 1)],
     "rounded8_1": [
@@ -115,9 +115,9 @@ def tile_picked_zkp_three_po_kernel(tc, x_words, x_scales, w1, w2, w3, corr, off
         load_w(2, 0, 2)
         load_corr(2, 3)
         load_w(2, 1, 2)
+        load_corr(1, 2)
         corr_rows = keep.tile([P, P], F32, name="corr_rows", align_bytes=64)
         nc.sync.dma_start(out=corr_rows[:], in_=corr[0:8, 0:8, :].rearrange("i r (h v) -> i (r h) v", h=HALVES))
-        load_corr(1, 2)
         load_w(4, 0, 2)
         load_w(4, 1, 2)
         load_both_passes(BY_UNIT)

@@ -386,6 +386,14 @@ def tile_picked_zkp_three_po_kernel(tc, x_words, x_scales, w1, w2, w3, corr, off
         turn_tile_back("a1", PACK)
         turn_tile_back("b0", PACK)
 
+        unit_a, unit_b = UNITS - 2, UNITS - 1
+        bank_a = sbanks.tile([P, HALVES, P], F32, name="sbank")
+        bank_b = [ybanks.tile([P, P], F32, name="ybank") for h in range(HALVES)]
+        for d in range(D - 1):
+            prod = prods.tile([P, V], F32, name="prod", align_bytes=64)
+            gather(prod[:], unit_a, d, 0, V)
+            for h in range(HALVES):
+                turn(bank_a[:, h, :], prod[:, h * P : (h + 1) * P], (d, h) == (0, 0), (d, h) == (D - 2, HALVES - 1))
         scale_pair(last_step)
         turn_tile_back("a2", 2)
         summed = [keep.tile([P, PACK, P], F32, name="summed%d" % h, align_bytes=64) for h in range(HALVES)]
@@ -397,15 +405,7 @@ def tile_picked_zkp_three_po_kernel(tc, x_words, x_scales, w1, w2, w3, corr, off
         out_rows = out_0.rearrange("(p t) v -> p t v", t=PACK)
         sums = keep.tile([P, PACK, V], F32, name="sums", align_bytes=64)
 
-        unit_a, unit_b = UNITS - 2, UNITS - 1
-        bank_a = sbanks.tile([P, HALVES, P], F32, name="sbank")
-        bank_b = [ybanks.tile([P, P], F32, name="ybank") for h in range(HALVES)]
-        for d in range(D - 1):
-            prod = prods.tile([P, V], F32, name="prod", align_bytes=64)
-            gather(prod[:], unit_a, d, 0, V)
-            for h in range(HALVES):
-                turn(bank_a[:, h, :], prod[:, h * P : (h + 1) * P], (d, h) == (0, 0), (d, h) == (D - 2, HALVES - 1))
-        prod = keep.tile([P, V], F32, name="prod", tag="last_prods", align_bytes=64)
+        prod = prods.tile([P, V], F32, name="prod", align_bytes=64)
         gather(prod[:], unit_b, 0, 0, V)
         for h in range(HALVES):
             turn(bank_b[h][:], prod[:, h * P : (h + 1) * P], True, False)

@@ -388,7 +388,6 @@ def tile_picked_zkp_three_po_kernel(tc, x_words, x_scales, w1, w2, w3, corr, off
 
         unit_a, unit_b = UNITS - 2, UNITS - 1
         bank_a = sbanks.tile([P, HALVES, P], F32, name="sbank")
-        bank_b = [ybanks.tile([P, P], F32, name="ybank") for h in range(HALVES)]
         for d in range(D - 1):
             prod = prods.tile([P, V], F32, name="prod", align_bytes=64)
             gather(prod[:], unit_a, d, 0, V)
@@ -405,28 +404,23 @@ def tile_picked_zkp_three_po_kernel(tc, x_words, x_scales, w1, w2, w3, corr, off
         out_rows = out_0.rearrange("(p t) v -> p t v", t=PACK)
         sums = keep.tile([P, PACK, V], F32, name="sums", align_bytes=64)
 
-        prod = prods.tile([P, V], F32, name="prod", align_bytes=64)
-        gather(prod[:], unit_b, 0, 0, V)
-        for h in range(HALVES):
-            turn(bank_b[h][:], prod[:, h * P : (h + 1) * P], True, False)
-        for h in range(HALVES):
-            prod = prods.tile([P, P], F32, name="prod", align_bytes=64)
-            gather(prod[:], unit_b, 1, h * P, (h + 1) * P)
-            turn(bank_b[h][:], prod[:], False, True)
         sums_a = keep.tile([P, HALVES, P], F32, name="first_sums", align_bytes=64)
         nc.scalar.copy(out=sums_a[:], in_=bank_a[:])
-        sums_b = [keep.tile([P, P], F32, name="last_sums%d" % h, align_bytes=64) for h in range(HALVES)]
         for h in range(HALVES):
-            turn_back(sums_a[:, h, :], 2, h, False)
-        for h in range(HALVES):
-            nc.scalar.copy(out=sums_b[h][:], in_=bank_b[h][:])
-            turn_back(sums_b[h][:], 3, h, h == HALVES - 1)
+            turn_back(sums_a[:, h, :], 2, h, h == HALVES - 1)
+        plain_a = keep.tile([P, V], F32, name="plain_a", tag="summed0", align_bytes=64)
+        nc.scalar.activation(plain_a[:], y[unit_a][:].indirect(pos_t[D - 1][:]), COPY)
         nc.scalar.activation(out=sums[:, 0:2, :], in_=planes[0][:], func=RELU)
         nc.sync.dma_start(out=out_rows[:, 0:2, :], in_=sums[:, 0:2, :])
+        terms_b = keep.tile([P, D + 1, V], F32, name="terms_b", align_bytes=64)
+        for d in range(D):
+            gather(terms_b[:, d, :], unit_b, d, 0, V)
         last_prods = keep.tile([P, 2, V], F32, name="last_prods", align_bytes=64)
-        gather(last_prods[:, 0, :], unit_a, D - 1, 0, V)
+        nc.vector.tensor_tensor(terms_b[:, D, :], terms_b[:, 0, :], terms_b[:, 1, :], ADD)
+        nc.vector.tensor_tensor(last_prods[:, 0, :], plain_a[:], near[entry(unit_a, D - 1)], MULT)
         for h in range(HALVES):
-            gather(last_prods[:, 1, h * P : (h + 1) * P], unit_b, D - 1, h * P, (h + 1) * P)
+            cols = slice(h * P, (h + 1) * P)
+            nc.vector.tensor_tensor(last_prods[:, 1, cols], terms_b[:, D, cols], terms_b[:, 2, cols], ADD)
 
         out_words = keep.tile([P, V], I32, name="out_words", align_bytes=64)
         out_planes = keep.tile([P, V], U8, name="out_planes", align_bytes=64)

@@ -219,8 +219,9 @@ def tile_picked_zkp_three_po_kernel(tc, x_words, x_scales, w1, w2, w3, corr, off
             round_pass(nc.scalar.copy, 0, g, 1)
             quantise(0, g)
         x_codes.append(keep.tile([P, S], I32, name="x_codes1", tag="raw0_1", align_bytes=64))
-        point_halves = [slice(j * S // 2, (j + 1) * S // 2) for j in range(2)]
-        first_product = [sbanks.tile([P, S // 2], F32, name="sbank") for j in range(2)]
+        point_halves = [slice(0, S // 2), slice(S // 2, 3 * S // 4), slice(3 * S // 4, S)]
+        first_product = [sbanks.tile([P, S // 2], F32, name="sbank"), sbanks.tile([P, S // 4], F32, name="sbank")]
+        first_product.append(banks.tile([P, S // 4], F32, name="first_rest", tag="planes1"))
         for g in range(PASSES):
             for j, points in enumerate(point_halves):
                 if g == PASSES - 1:

from contextlib import ExitStack

import concourse.mybir as mybir
from concourse.masks import make_identity

F32 = mybir.dt.float32
BF16 = mybir.dt.bfloat16
I32 = mybir.dt.int32
U32 = mybir.dt.uint32
U16 = mybir.dt.uint16
U8 = mybir.dt.uint8
FP8X4 = mybir.dt.float8_e4m3fn_x4
RELU = mybir.ActivationFunctionType.Relu
COPY = mybir.ActivationFunctionType.Copy
MULT = mybir.AluOpType.mult
ADD = mybir.AluOpType.add

K, T, S, D, V, N = 1024, 1024, 512, 3, 256, 512
P = 128
PACK = 4
PASS_ROWS = P * PACK
PASSES = K // PASS_ROWS
CHUNKS = N // P
HALVES = V // P
LINE = 4
FLOPS = 2 * K * N * S * D

UNITS = D * CHUNKS
DEALT_FROM = (D - 1) * CHUNKS
PAIRS = UNITS // 2
BY_UNIT = 6

SCALED = ((1,), (3,), (4,), (6,), ())
WEIGHED = (0, 5)
PUT_OFF = (5, 2)

WAITS = {
    "raw2_1": [("fetch", 1, 0), ("fetch", 1, 1), ("fused", 1, 2)],
    "raw4_1": [("fetch", 3, 0), ("fetch", 3, 1), ("fused", 2, 1), ("fused", 3, 2)],
    "rounded6_1": [("fetch", 5, 0), ("fetch", 4, 1), ("fetch", 5, 1)],
    "rounded8_1": [
        ("fused", 6, 2),
        ("fused", 7, 2),
        ("fused", 7, 1),
        ("fetch", 7, 0),
        ("fetch", 6, 1),
        ("weigh", 5, 1),
        ("fused", 5, 2),
    ],
}
HELD_CODES_OFFSET = PACK * N * 4 - 2 * P * 4


def tile_picked_zkp_three_po_kernel(tc, x_words, x_scales, w1, w2, w3, corr, offs, pos1, pos2, pos3, out_0, out_1, out_2):
    nc = tc.nc
    weights = [w1, w2, w3]
    with ExitStack() as ctx:
        lists = ctx.enter_context(tc.tile_pool(name="lists", bufs=1))
        keep = ctx.enter_context(tc.tile_pool(name="keep", bufs=1))
        placed = ctx.enter_context(tc.tile_pool(name="placed", bufs=1))
        prods = ctx.enter_context(tc.tile_pool(name="prods", bufs=D * UNITS + 2))
        ybanks = ctx.enter_context(tc.psum_pool(name="ybanks", bufs=2))
        sbanks = ctx.enter_context(tc.psum_pool(name="sbanks", bufs=2))
        banks = ctx.enter_context(tc.psum_pool(name="banks", bufs=1))

        offs_t = lists.tile([P, S // 16], U16, name="offs_t")
        pos_t = [lists.tile([P, V // 16], U16, name="pos_t%d" % d) for d in range(D)]
        x_all = [keep.tile([P, T], I32, name="x_all%d" % g, align_bytes=64) for g in range(PASSES)]
        xs_all = keep.tile([P, T], U8, name="xs_all", align_bytes=64)
        near = {}
        loaded = {}

        def load_x(g):
            nc.sync.dma_start(out=x_all[g][:], in_=x_words[g].rearrange("p n t -> p (n t)").bitcast(I32))

        def weight_rows(u, g, count):
            q, c = divmod(u, CHUNKS)
            part = weights[q][g * PASS_ROWS : (g + 1) * PASS_ROWS, c * P : (c + count) * P]
            return part.rearrange("(p t) n -> p t n", t=PACK)

        def load_w(u, g, count):
            if (u, g) == (DEALT_FROM, 1):
                tile = placed.tile([P, PACK, count * P], F32, name="last_raw", align_bytes=64, offset=0)
            else:
                tile = keep.tile([P, PACK, count * P], F32, name="raw", tag="raw%d_%d" % (u, g), align_bytes=64)
            nc.sync.dma_start(out=tile[:], in_=weight_rows(u, g, count))
            loaded[(u, g)] = tile

        def load_both_passes(u):
            loaded[u] = keep.tile([P, PASSES, PACK, 2 * P], F32, name="raw", tag="raw%d_1" % u, align_bytes=64)
            for g in range(PASSES):
                nc.sync.dma_start(out=loaded[u][:, g], in_=weight_rows(u, g, 2))

        def load_corr(lo, hi):
            tile = keep.tile([P, hi - lo, V], F32, name="corr%d" % lo, align_bytes=64)
            nc.sync.dma_start(out=tile[:], in_=corr[lo:hi].rearrange("d p v -> p d v"))
            for i in range(lo, hi):
                near[i] = tile[:, i - lo, :]

        nc.gpsimd.memset(xs_all[:].bitcast(I32), 0)
        nc.sync.dma_start(offs_t[:], offs)
        load_x(0)
        for quad in range(4):
            nc.sync.dma_start(
                out=xs_all[32 * quad : 32 * quad + 4 * PASSES, :].bitcast(I32),
                in_=x_scales[:, 4 * quad : 4 * quad + 4, :].bitcast(I32),
            )
        load_w(0, 0, 1)
        load_w(0, 1, 1)
        load_x(1)
        load_w(1, 0, 1)
        load_w(1, 1, 1)
        for d, pos in enumerate((pos1, pos2, pos3)):
            nc.sync.dma_start(pos_t[d][:], pos)
        load_w(2, 0, 2)
        load_corr(2, 3)
        load_w(2, 1, 2)
        load_corr(1, 2)
        corr_rows = keep.tile([P, P], F32, name="corr_rows", align_bytes=64)
        nc.sync.dma_start(out=corr_rows[:], in_=corr[0:8, 0:8, :].rearrange("i r (h v) -> i (r h) v", h=HALVES))
        load_w(4, 0, 2)
        load_w(4, 1, 2)
        load_both_passes(BY_UNIT)
        load_corr(4, 6)
        for g in range(PASSES):
            load_w(DEALT_FROM, g, CHUNKS)
        load_corr(6, 9)

        ident = keep.tile([P, P], F32, name="ident")
        make_identity(nc, ident[:])

        def turn(target, block, first, final):
            nc.tensor.matmul(out=target, lhsT=block, rhs=ident[:], is_transpose=True, start=first, stop=final)

        x_codes = [keep.tile([P, S], I32, name="x_codes0", align_bytes=64)]
        x_planes = keep.tile([P, S], U8, name="x_planes", align_bytes=64)
        nc.vector.tensor_copy(x_codes[0][:].bitcast(U32), x_all[0][:].bitcast(U32).indirect(offs_t[:]))
        nc.vector.tensor_copy(x_planes[:], xs_all[:].indirect(offs_t[:]))

        rounded = {}
        codes = {}
        ybank = {}
        y = {}

        def round_pass(copy, u, g, count):
            rounded[(u, g)] = keep.tile([P, count * P, PACK], BF16, name="rounded", tag="rounded%d_%d" % (u, g), align_bytes=64)
            copy(
                out=rounded[(u, g)][:].rearrange("p (c i) t -> p c t i", i=LINE),
                in_=loaded[(u, g)][:].rearrange("p t (c i) -> p c t i", i=LINE),
            )

        def dealt_views(u, g):
            s = u - DEALT_FROM
            target = rounded[(u, g)][:].rearrange("p (s m) t -> p m t s", s=2)
            source = loaded[(DEALT_FROM, g)][:].rearrange("p t (m s) -> p m t s", s=PACK)[:, :, :, s : s + 2]
            return target, source

        def round_dealt(u, g):
            rounded[(u, g)] = keep.tile([P, 2 * P, PACK], BF16, name="rounded", tag="rounded%d_%d" % (u, g), align_bytes=64)
            target, source = dealt_views(u, g)
            nc.vector.tensor_copy(out=target, in_=source)

        def round_last(half):
            if half == 0:
                rounded[(UNITS - 2, 1)] = keep.tile([P, 2 * P, PACK], BF16, name="rounded_last", align_bytes=64)
            rows = slice(half * P // 2, (half + 1) * P // 2)
            target, source = dealt_views(UNITS - 2, 1)
            nc.vector.tensor_copy(out=target[:, rows], in_=source[:, rows])

        def round_unit(u, j):
            rounded[(u, j)] = keep.tile([P, PASSES * P, PACK], BF16, name="rounded", tag="rounded%d_%d" % (u, j), align_bytes=64)
            nc.vector.tensor_copy(
                out=rounded[(u, j)][:].rearrange("p (g c i) t -> p g c t i", g=PASSES, i=LINE),
                in_=loaded[u][:, :, :, j * P : (j + 1) * P].rearrange("p g t (c i) -> p g c t i", i=LINE),
            )

        def quantise(u, part):
            width = rounded[(u, part)].shape[1]
            if (u, part) == (UNITS - 2, 0):
                w_codes = placed.tile([P, width], I32, name="held_codes", align_bytes=64, offset=HELD_CODES_OFFSET)
            else:
                w_codes = keep.tile([P, width], I32, name="w_codes", tag="w_codes%d_%d" % (u, part), align_bytes=64)
            w_planes = keep.tile([P, width], U8, name="w_planes", tag="w_planes%d_%d" % (u, part), align_bytes=64)
            nc.vector.quantize_mx(
                out=w_codes[:].bitcast(FP8X4), scales=w_planes[:], in_=rounded[(u, part)][:].rearrange("p c t -> p (c t)")
            )
            for j in range(width // P):
                key = (u + part, j) if u == BY_UNIT else (u + j, part)
                codes[key] = (w_codes[:, j * P : (j + 1) * P], w_planes[:, j * P : (j + 1) * P])

        def one_pass(bank, u, g, points):
            w_codes, w_planes = codes[(u, g)]
            nc.tensor.matmul_mx(
                out=bank,
                lhsT=w_codes.bitcast(FP8X4),
                lhsT_scale=w_planes,
                rhs=x_codes[g][:, points].bitcast(FP8X4),
                rhs_scale=x_planes[4 * g : P, points],
                start=(g == 0),
                stop=(g == PASSES - 1),
            )

        def multiply(u):
            ybank[u] = ybanks.tile([P, S], F32, name="ybank")
            for g in range(PASSES):
                one_pass(ybank[u][:], u, g, slice(0, S))

        def unload(u):
            y[u] = keep.tile([P, S], F32, name="y", tag="y%d" % u, align_bytes=64)
            nc.scalar.copy(out=y[u][:], in_=ybank[u][:])

        def entry(u, d):
            return D * (u // CHUNKS) + d

        def gather(prod, u, d, lo, hi):
            nc.vector.tensor_tensor(prod, y[u][:].indirect(pos_t[d][:, lo // 16 : hi // 16]), near[entry(u, d)][:, lo:hi], MULT)

        for g in range(PASSES):
            round_pass(nc.scalar.copy, 0, g, 1)
            quantise(0, g)
        x_codes.append(keep.tile([P, S], I32, name="x_codes1", tag="raw0_1", align_bytes=64))
        point_halves = [slice(0, S // 2), slice(S // 2, 3 * S // 4), slice(3 * S // 4, S)]
        first_product = [sbanks.tile([P, S // 2], F32, name="sbank"), sbanks.tile([P, S // 4], F32, name="sbank")]
        first_product.append(banks.tile([P, S // 4], F32, name="first_rest", tag="planes1"))
        for g in range(PASSES):
            for j, points in enumerate(point_halves):
                if g == PASSES - 1:
                    half_list = offs_t[:, points.start // 16 : points.stop // 16]
                    nc.vector.tensor_copy(x_codes[g][:, points].bitcast(U32), x_all[g][:].bitcast(U32).indirect(half_list))
                one_pass(first_product[j][:], 0, g, points)
        round_pass(nc.scalar.copy, 1, 0, 1)
        round_pass(nc.vector.tensor_copy, 1, 1, 1)
        y[0] = keep.tile([P, S], F32, name="y", tag="y0", align_bytes=64)
        for j, points in enumerate(point_halves):
            nc.scalar.copy(out=y[0][:, points], in_=first_product[j][:])
        quantise(1, 0)
        quantise(1, 1)
        multiply(1)

        rows_turned = banks.tile([P, P], F32, name="rows_turned", tag="planes0")
        turn(rows_turned[:], corr_rows[:], True, True)
        near_cols = keep.tile([P, 8, HALVES], F32, name="near_cols", align_bytes=64)
        nc.scalar.copy(out=near_cols[:], in_=rows_turned[:].rearrange("v (i r h) -> v i r h", i=8, h=HALVES)[:, :, 0, :])

        wide = [banks.tile([P, N], F32, name="acc%d" % h, tag="acc%d" % h) for h in range(HALVES)]
        planes = [banks.tile([P, 2, V], F32, name="planes%d" % a, tag="planes%d" % a) for a in range(2)]
        opened = set()
        fetched_banks = {}
        scaled = {}
        plain = {}
        waiting = {}

        def opens(group):
            fresh = group not in opened
            opened.add(group)
            return fresh

        def buffer_for(*term):
            for tag, terms in WAITS.items():
                if term in terms:
                    if tag not in waiting:
                        waiting[tag] = keep.tile([P, len(terms), V], F32, name="later", tag=tag, align_bytes=64)
                    return waiting[tag][:, terms.index(term), :]
            return prods.tile([P, V], F32, name="prod", align_bytes=64)[:]

        def turn_back(tile, t, h, final):
            turn(planes[t // 2][:, t % 2, h * P : (h + 1) * P], tile, opens(("planes", t // 2)), final)

        def fetch(u, d):
            target = buffer_for("fetch", u, d)
            nc.scalar.activation(target, y[u][:].indirect(pos_t[d][:]), COPY)
            return target

        def fetch_and_turn(u, d, bank, first, final):
            values = fetch(u, d)
            for h in range(HALVES):
                turn(bank[:, h, :], values[:, h * P : (h + 1) * P], first and h == 0, final and h == HALVES - 1)

        def fetch_pair(pair):
            firsts = sbanks.tile([P, HALVES, 2, P], F32, name="sbank")
            extra = SCALED[pair]
            seconds = sbanks.tile([P, HALVES, len(extra), P], F32, name="sbank") if extra else None
            terms = [(2 * pair, 0), (2 * pair + 1, 0)] + [(u, 1) for u in extra]
            terms = terms + [(u, 1) for u in WEIGHED if u // 2 == pair]
            if pair == 0:
                terms = sorted(terms)
            for u, d in terms:
                if d == 0:
                    fetch_and_turn(u, d, firsts[:, :, u % 2, :], u % 2 == 0, u % 2 == 1)
                elif u in WEIGHED:
                    plain[u] = fetch(u, d)
                else:
                    fetch_and_turn(u, d, seconds[:, :, 0, :], True, True)
            fetched_banks[pair] = (firsts, seconds)

        def add_wide(prod, u, final):
            for h in range(HALVES):
                block = prod[:, h * P : (h + 1) * P]
                if u < DEALT_FROM:
                    c = u % CHUNKS
                    turn(wide[h][:, c * P : (c + 1) * P], block, opens(("wide", h)), False)
                else:
                    turn(wide[h][:].rearrange("v (p t) -> v t p", t=PACK)[:, u - DEALT_FROM, :], block, False, final)

        def weigh_pair(pair):
            for u in WEIGHED:
                if u // 2 == pair:
                    prod = buffer_for("weigh", u, 1)
                    nc.vector.tensor_tensor(prod, plain[u], near[entry(u, 1)], MULT)
                    add_wide(prod, u, False)

        def by_plane(target, source):
            return target.rearrange("v (a e) p -> v a p e", e=2), source.rearrange("v (p a e) -> v a p e", a=2, e=2)

        def scale(key, bank, u, count, d):
            if key not in scaled:
                scaled[key] = keep.tile([P, HALVES, PACK, P], F32, name="scaled%s" % key, align_bytes=64)
            c = u % CHUNKS
            for h in range(HALVES):
                if u < DEALT_FROM:
                    rows = slice(c * P // PACK, (c + count) * P // PACK)
                    target, source = by_plane(scaled[key][:, h, :, rows], bank[:, h])
                else:
                    target, source = scaled[key][:, h, c : c + count, :].rearrange("v t p -> v (t p)"), bank[:, h]
                nc.scalar.activation(target, source, COPY, scale=near_cols[:, entry(u, d), h : h + 1])

        def scale_pair(pair):
            firsts, seconds = fetched_banks[pair]
            scale("a%d" % (pair // 2), firsts[:].rearrange("v h j m -> v h (j m)"), 2 * pair, 2, 0)
            if SCALED[pair]:
                scale("b0", seconds[:].rearrange("v h j m -> v h (j m)"), SCALED[pair][0], 1, 1)

        def turn_tile_back(key, count):
            for h in range(HALVES):
                for t in range(count):
                    turn_back(scaled[key][:, h, t, :], t, h, False)

        last_step = PAIRS - 2
        for p in range(PAIRS - 1):
            u = 2 * p
            ahead = u + 2
            fused = [term for term in [(u, 2), (u, 1), (u + 1, 2), (u + 1, 1)] if term != PUT_OFF]
            fused = [term for term in fused if term[1] == 2 or term[0] not in SCALED[p] + WEIGHED]
            if p == PUT_OFF[0] // 2 + 1:
                fused.append(PUT_OFF)
            if ahead == BY_UNIT:
                round_unit(ahead, 0)
                round_unit(ahead, 1)
            elif ahead < DEALT_FROM:
                round_pass(nc.vector.tensor_copy, ahead, 0, 2)
                round_pass(nc.vector.tensor_copy, ahead, 1, 2)
            elif ahead == DEALT_FROM:
                round_dealt(ahead, 0)
                round_dealt(ahead + 2, 0)
                round_dealt(ahead, 1)
            if p < last_step:
                quantise(ahead, 0)
            if ahead == DEALT_FROM:
                round_last(0)
            if p > 0:
                unload(u)
            unload(u + 1)
            if p > 0:
                scale_pair(p - 1)
            if p < last_step:
                quantise(ahead, 1)
            if ahead == DEALT_FROM:
                round_last(1)
            for j in range(2):
                multiply(ahead + j)
                if p == last_step:
                    unload(ahead + j)
            fetch_pair(p)
            if p == CHUNKS // 2:
                turn_tile_back("a0", PACK)
            for k, (unit, d) in enumerate(fused):
                prod = buffer_for("fused", unit, d)
                gather(prod, unit, d, 0, V)
                add_wide(prod, unit, (p, k) == (last_step, len(fused) - 1))
                if k == 0 and p > 1:
                    weigh_pair(p - 1)
                if (p, k) == (0, len(fused) - 1):
                    weigh_pair(0)
                if k == 0 and ahead == DEALT_FROM:
                    for g in range(PASSES):
                        quantise(ahead + 2, g)
        turn_tile_back("a1", PACK)
        turn_tile_back("b0", PACK)

        unit_a, unit_b = UNITS - 2, UNITS - 1
        bank_a = sbanks.tile([P, HALVES, P], F32, name="sbank")
        for d in range(D - 1):
            prod = prods.tile([P, V], F32, name="prod", align_bytes=64)
            gather(prod[:], unit_a, d, 0, V)
            for h in range(HALVES):
                turn(bank_a[:, h, :], prod[:, h * P : (h + 1) * P], (d, h) == (0, 0), (d, h) == (D - 2, HALVES - 1))
        scale_pair(last_step)
        turn_tile_back("a2", 2)
        summed = [keep.tile([P, PACK, P], F32, name="summed%d" % h, align_bytes=64) for h in range(HALVES)]
        for h in range(HALVES):
            target, source = by_plane(summed[h][:], wide[h][:])
            nc.scalar.copy(out=target, in_=source)
            for t in range(PACK):
                turn_back(summed[h][:, t, :], t, h, (t, h) == (1, HALVES - 1))
        out_rows = out_0.rearrange("(p t) v -> p t v", t=PACK)
        sums = keep.tile([P, PACK, V], F32, name="sums", align_bytes=64)

        sums_a = keep.tile([P, HALVES, P], F32, name="first_sums", align_bytes=64)
        nc.scalar.copy(out=sums_a[:], in_=bank_a[:])
        for h in range(HALVES):
            turn_back(sums_a[:, h, :], 2, h, h == HALVES - 1)
        plain_a = keep.tile([P, V], F32, name="plain_a", tag="summed0", align_bytes=64)
        nc.scalar.activation(plain_a[:], y[unit_a][:].indirect(pos_t[D - 1][:]), COPY)
        nc.scalar.activation(out=sums[:, 0:2, :], in_=planes[0][:], func=RELU)
        nc.sync.dma_start(out=out_rows[:, 0:2, :], in_=sums[:, 0:2, :])
        terms_b = keep.tile([P, D + 1, V], F32, name="terms_b", align_bytes=64)
        for d in range(D):
            gather(terms_b[:, d, :], unit_b, d, 0, V)
        last_prods = keep.tile([P, 2, V], F32, name="last_prods", align_bytes=64)
        nc.vector.tensor_tensor(terms_b[:, D, :], terms_b[:, 0, :], terms_b[:, 1, :], ADD)
        nc.vector.tensor_tensor(last_prods[:, 0, :], plain_a[:], near[entry(unit_a, D - 1)], MULT)
        for h in range(HALVES):
            cols = slice(h * P, (h + 1) * P)
            nc.vector.tensor_tensor(last_prods[:, 1, cols], terms_b[:, D, cols], terms_b[:, 2, cols], ADD)

        out_words = keep.tile([P, V], I32, name="out_words", align_bytes=64)
        out_planes = keep.tile([P, V], U8, name="out_planes", align_bytes=64)
        result_bf = keep.tile([P, V, PACK], BF16, name="result_bf", align_bytes=64)
        late = keep.tile([P, 2, V], F32, name="late", align_bytes=64)
        centre_halves = [slice(h * P, (h + 1) * P) for h in range(HALVES)]
        for cols in centre_halves:
            nc.vector.tensor_tensor(sums[:, 2:4, cols], last_prods[:, :, cols], planes[1][:, :, cols], ADD)
        for cols in centre_halves:
            nc.vector.tensor_scalar_max(
                result_bf[:, cols, :].rearrange("p (c i) t -> p c t i", i=LINE),
                sums[:, :, cols].rearrange("p t (c i) -> p c t i", i=LINE),
                0.0,
            )
        for cols in centre_halves:
            nc.scalar.activation(out=late[:, :, cols], in_=sums[:, 2:4, cols], func=RELU)
            nc.sync.dma_start(out=out_rows[:, 2:4, cols], in_=late[:, :, cols])
        for cols in centre_halves:
            nc.vector.quantize_mx(
                out=out_words[:, cols].bitcast(FP8X4), scales=out_planes[:, cols], in_=result_bf[:, cols, :].rearrange("p c t -> p (c t)")
            )
            nc.scalar.dma_start(out=out_1[0].rearrange("p c r -> p (c r)").bitcast(I32)[:, cols], in_=out_words[:, cols])
        for quad in range(4):
            queue = nc.scalar if quad % 2 else nc.sync
            queue.dma_start(
                out=out_2[0][4 * quad : 4 * quad + 4, :].bitcast(I32), in_=out_planes[32 * quad : 32 * quad + 4, :].bitcast(I32)
            )
